import numpy as np
import ml_dtypes


def mxq(x, axis, fmt="e4m3"):
    dtype, down = {"e4m3": (ml_dtypes.float8_e4m3fn, 7), "e5m2": (ml_dtypes.float8_e5m2, 14)}[fmt]
    v = np.moveaxis(np.asarray(x, np.float32).astype(ml_dtypes.bfloat16).astype(np.float64), axis, -1)
    blocks = v.reshape(v.shape[:-1] + (-1, 32))
    amax = np.abs(blocks).max(-1, keepdims=True)
    byte = np.maximum(np.where(amax > 0, np.frexp(amax)[1] - 1 + 127, 0) - down, 1)
    scale = np.exp2(byte - 127.0)
    codes = (blocks / scale).astype(np.float32).astype(dtype).astype(np.float64)
    return np.moveaxis((codes * scale).reshape(v.shape), -1, axis)


WIDE = False


def mx_kscale(k):
    if not WIDE:
        return np.ones(k)
    levels = np.array([10, -10, 5, -5, 0])
    if k % 512:
        return np.exp2(np.random.permutation(np.resize(levels, k // 32))).repeat(32)
    a = np.empty((k // 512, 16))
    for p in range(k // 512):
        a[p, :8] = np.random.permutation(np.resize(levels, 8))
        for g in range(8):
            far = levels[np.abs(levels - a[p, g]) >= 10]
            a[p, g + 8] = far[np.random.randint(len(far))]
    return np.exp2(a.ravel()).repeat(32)


def f64(x):
    return np.asarray(x).astype(np.float64)


def striped(idx):
    return np.tile(np.asarray(idx).reshape(-1, 16).T, (8, 1)).astype(np.uint16)


def unstriped(offs):
    return offs[:16].T.reshape(-1).astype(np.int64)


E2M1 = np.array([0.0, 0.5, 1.0, 1.5, 2.0, 3.0, 4.0, 6.0, -0.0, -0.5, -1.0, -1.5, -2.0, -3.0, -4.0, -6.0])


def pack_weight(w, fmt):
    k, n = w.shape
    w = f64(np.asarray(w, np.float32).astype(ml_dtypes.bfloat16)).reshape(k // 32, 32, n)
    amax = np.abs(w).max(1)
    if fmt == "e4m3":
        byte = np.frexp(amax)[1] - 1 + 127 - 7
    else:
        mant, ex = np.frexp(amax / 6.0)
        byte = np.where(mant > 0.5, ex, ex - 1) + 127
    byte = np.clip(np.where(amax > 0, byte, 1), 1, 254)
    scaled = (w * np.exp2(127.0 - byte)[:, None, :]).reshape(k, n).astype(np.float32)
    by_word = np.ascontiguousarray(scaled.reshape(k // 512, 128, 4, n).transpose(0, 1, 3, 2))
    if fmt == "e4m3":
        words = by_word.astype(ml_dtypes.float8_e4m3fn).view(np.uint8)
    else:
        c = by_word.astype(ml_dtypes.float4_e2m1fn).view(np.uint8) & 0xF
        words = (c[..., 0::2] | (c[..., 1::2] << 4)).reshape(k // 512, 128, 2 * n)
    return np.ascontiguousarray(words), np.ascontiguousarray(byte.astype(np.uint8).reshape(k // 512, 16, n))


def unpack_weight(words, scales, fmt):
    g, _, n = scales.shape
    words = np.ascontiguousarray(words).reshape(g, 128, n, -1)
    if fmt == "e4m3":
        vals = words.view(ml_dtypes.float8_e4m3fn).astype(np.float64)
    else:
        nib = np.empty((g, 128, n, 4), np.uint8)
        nib[..., 0::2] = words & 0xF
        nib[..., 1::2] = words >> 4
        vals = E2M1[nib]
    vals = vals * np.repeat(np.exp2(scales.astype(np.float64) - 127.0), 8, axis=1)[..., None]
    return vals.transpose(0, 1, 3, 2).reshape(g * 512, n)


B, N, T, D, NQ = 1, 512, 2048, 1024, 512
DV = 512


def sgn(shape):
    return np.random.uniform(0.5, 2.0, shape) * np.where(np.random.standard_normal(shape) < 0, -1.0, 1.0)


def setup_inputs():
    n = np.random.standard_normal
    idx = np.random.permutation(T)[:B * N]
    s = mx_kscale(D)[:, None]
    u = mx_kscale(N)
    ut = np.ones(T)
    ut[idx] = u
    kp = pack_weight(n((D, T)) / s, "e2m1")
    cp = pack_weight(n((D, T)) / s / 12, "e2m1")
    return {
        "qT": (n((B, D, NQ)) * s * (1.00 / np.sqrt(D))).astype(np.float32),
        "k_words": np.ascontiguousarray(kp[0].reshape(1, 2, 128, T, 2).transpose(0, 2, 3, 1, 4)).reshape(1, 128, T, 4),
        "k_scales": kp[1],
        "c_words": np.ascontiguousarray(cp[0].reshape(1, 2, 128, T, 2).transpose(0, 2, 3, 1, 4)).reshape(1, 128, T, 4),
        "c_scales": cp[1],
        "vT": (n((DV, T)) / ut).astype(np.float32),
        "ls": (np.random.uniform(7.0, 7.6, (B, 1, NQ))).astype(np.float32),
        "us": (sgn((B, N, 1)) * u[:, None]).astype(np.float32),
        "offs": striped(idx),
    }


def reference(qT, k_words, k_scales, c_words, c_scales, vT, ls, us, offs):
    idx = unstriped(offs)
    pick = lambda x, which: x[:, which].reshape(x.shape[0], B, -1).transpose(1, 0, 2)
    k = unpack_weight(k_words.reshape(1, 128, T, 2, 2).transpose(0, 3, 1, 2, 4).reshape(2, 128, 2 * T), k_scales, "e2m1")
    kg = pick(k, idx)
    c = unpack_weight(c_words.reshape(1, 128, T, 2, 2).transpose(0, 3, 1, 2, 4).reshape(2, 128, 2 * T), c_scales, "e2m1")
    cg = pick(c, idx)
    qq = mxq(f64(qT), 1, "e4m3")
    a = (kg.transpose(0, 2, 1) @ qq) + (cg.transpose(0, 2, 1) @ qq)
    y = np.exp(a - f64(ls)) * f64(us)
    wq = mxq(y, 1, "e4m3")
    o = wq.transpose(0, 2, 1) @ mxq(pick(f64(vT), idx).transpose(0, 2, 1), 1, "e4m3")
    return o

@@ -1,0 +1,183 @@
+from contextlib import ExitStack
+
+import concourse.mybir as mybir
+from concourse.masks import make_identity
+
+F32 = mybir.dt.float32
+BF16 = mybir.dt.bfloat16
+I32 = mybir.dt.int32
+U32 = mybir.dt.uint32
+U16 = mybir.dt.uint16
+U8 = mybir.dt.uint8
+FP8X4 = mybir.dt.float8_e4m3fn_x4
+FP4X4 = mybir.dt.float4_e2m1fn_x4
+EXP = mybir.ActivationFunctionType.Exp
+MULT = mybir.AluOpType.mult
+
+P = 128
+PACK = 4
+N, T, D, NQ, DV = 512, 2048, 1024, 512, 512
+PASSES = D // (P * PACK)
+Q_HALVES = 2
+Q_HALF = NQ // Q_HALVES
+Q_TILES = NQ // P
+E_TILES = DV // P
+SHIFT = 16
+
+FLOPS = 2 * N * NQ * (2 * D + DV)
+
+
+def tile_attend_at_resid_topk_kernel(tc, qT, k_words, k_scales, c_words, c_scales, vT, ls, us, offs, out):
+    nc = tc.nc
+    with ExitStack() as ctx:
+        keep = ctx.enter_context(tc.tile_pool(name="keep", bufs=1))
+        ring = ctx.enter_context(tc.tile_pool(name="ring", bufs=2))
+        psum = ctx.enter_context(tc.psum_pool(name="psum", bufs=1))
+
+        offsets = keep.tile([P, N // 16], U16, name="offsets")
+        nc.sync.dma_start(offsets[:], offs)
+
+        tables = (("k", k_words, k_scales), ("c", c_words, c_scales))
+
+        q_raw = []
+        for o in range(PASSES):
+            raw = keep.tile([P, PACK, NQ], F32, name="q_raw_%d" % o, tag="stage_%d" % o)
+            rows = qT[0, o * P * PACK : (o + 1) * P * PACK, :]
+            nc.sync.dma_start(raw[:], rows.rearrange("(p j) c -> p j c", j=PACK))
+            q_raw.append(raw)
+
+        byte_pools = []
+        for i, (name, words, scales) in enumerate(tables):
+            pool_bytes = keep.tile([P, T], U8, name=name + "_pool_bytes", tag="stage_%d" % (PASSES + i))
+            (nc.vector, nc.gpsimd)[i].memset(pool_bytes[:].bitcast(I32), 0)
+            rows = scales.rearrange("o (a r) t -> r a o t", r=4)
+            for r in range(4):
+                queue = nc.gpsimd if (i == 1 and r >= 2) else nc.scalar
+                queue.dma_start(pool_bytes[r:P:SHIFT, :].bitcast(I32), rows[r].bitcast(I32))
+            byte_pools.append(pool_bytes)
+
+        identity = keep.tile([P, P], F32, name="identity")
+        make_identity(nc, identity[:])
+
+        ls_cols = keep.tile([P, Q_TILES], F32, name="ls_cols")
+        with nc.allow_non_contiguous_dma(reason="one log-sum-exp a partition"):
+            nc.gpsimd.dma_start(ls_cols[:], ls[0, 0].rearrange("(m p) -> p m", p=P))
+        us_cols = keep.tile([P, PACK], F32, name="us_cols")
+        nc.gpsimd.dma_start(us_cols[:], us[0].rearrange("(p t) one -> p (t one)", t=PACK))
+        neg_ls = keep.tile([P, Q_TILES], F32, name="neg_ls")
+        nc.gpsimd.tensor_scalar_mul(neg_ls[:], ls_cols[:], -1.0)
+
+        key_planes = []
+        for (name, words, scales), pool_bytes in zip(tables, byte_pools):
+            listed_bytes = keep.tile([P, N], U8, name=name + "_listed_bytes", align_bytes=64)
+            nc.vector.tensor_copy(listed_bytes[:], pool_bytes[:].indirect(offsets[:]))
+            moved_bytes = keep.tile([P, N], U8, name=name + "_moved_bytes", align_bytes=64)
+            nc.vector.memset(moved_bytes[:].bitcast(I32), 0)
+            nc.sync.dma_start(moved_bytes[0 : P - SHIFT, :].bitcast(I32), listed_bytes[SHIFT:P, :].bitcast(I32))
+            key_planes.append((listed_bytes, moved_bytes))
+
+        word_pools = []
+        for i, (name, words, scales) in enumerate(tables):
+            pool_words = keep.tile([P, T], I32, name=name + "_pool_words", tag="stage_%d" % (PASSES + i))
+            nc.sync.dma_start(pool_words[:], words[0].rearrange("p t b -> p (t b)").bitcast(I32))
+            word_pools.append(pool_words)
+
+        q_mx = {}
+        for o in range(PASSES):
+            for h in range(Q_HALVES):
+                grouped = keep.tile([P, Q_HALF, PACK], BF16, name="q_grouped_%d_%d" % (h, o), align_bytes=64)
+                part = q_raw[o][:, :, h * Q_HALF : (h + 1) * Q_HALF].rearrange("p j c -> p c j")
+                if o == 0:
+                    nc.vector.tensor_copy(grouped[:], part)
+                else:
+                    nc.scalar.copy(grouped[:], part)
+                codes = keep.tile([P, Q_HALF], U32, name="q_codes_%d_%d" % (h, o), align_bytes=64)
+                plane = keep.tile([P, Q_HALF], U8, name="q_plane_%d_%d" % (h, o), align_bytes=64)
+                nc.vector.quantize_mx(out=codes[:].bitcast(FP8X4), scales=plane[:], in_=grouped[:].rearrange("p c j -> p (c j)"))
+                q_mx[h, o] = (codes, plane)
+
+        key_codes = []
+        for (name, words, scales), pool_words in zip(tables, word_pools):
+            listed_words = keep.tile([P, N], U32, name=name + "_listed_words", align_bytes=64)
+            nc.vector.tensor_copy(listed_words[:], pool_words[:].bitcast(U32).indirect(offsets[:]))
+            halves = keep.tile([P, PASSES, N], U16, name=name + "_halves", align_bytes=64)
+            nc.vector.tensor_copy(halves[:], listed_words[:].bitcast(U16).rearrange("p (n o) -> p o n", o=PASSES))
+            key_codes.append(halves)
+
+        v_pools = []
+        for j in range(E_TILES):
+            v_pool = keep.tile([P, T], F32, name="v_pool_%d" % j, tag="stage_%d" % j)
+            nc.sync.dma_start(v_pool[:], vT[j * P : (j + 1) * P, :])
+            v_pools.append(v_pool)
+
+        banks = [psum.tile([P, N], F32, name="scores_%d" % m) for m in range(Q_TILES)]
+
+        def score_pass(m, table, o):
+            h, cols = divmod(m * P, Q_HALF)
+            codes, plane = q_mx[h, o]
+            nc.tensor.matmul_mx(
+                out=banks[m][:],
+                lhsT=codes[:, cols : cols + P].bitcast(FP8X4),
+                lhsT_scale=plane[:, cols : cols + P],
+                rhs=key_codes[table][:, o, :].bitcast(FP4X4),
+                rhs_scale=key_planes[table][o][:],
+                start=(table == 0 and o == 0),
+                stop=(table == len(tables) - 1 and o == PASSES - 1),
+            )
+
+        for o in range(PASSES):
+            for m in range(Q_TILES):
+                score_pass(m, 0, o)
+
+        y_mx = []
+        for m in range(Q_TILES):
+            for o in range(PASSES):
+                score_pass(m, 1, o)
+            dealt = ring.tile([P, PACK, P], F32, name="dealt")
+            nc.scalar.activation(dealt[:], banks[m][:].rearrange("q (s t) -> q t s", t=PACK), EXP, bias=neg_ls[:, m : m + 1])
+            turned = psum.tile([P, PACK, P], F32, name="turned", bufs=2)
+            for t in range(PACK):
+                nc.tensor.transpose(turned[:, t, :], dealt[:, t, :], identity[:])
+            grouped = ring.tile([P, P, PACK], BF16, name="y_grouped", align_bytes=64)
+            nc.vector.tensor_tensor(
+                grouped[:],
+                turned[:].rearrange("s t q -> s q t"),
+                us_cols[:].unsqueeze(1).to_broadcast([P, P, PACK]),
+                MULT,
+            )
+            codes = keep.tile([P, P], U32, name="y_codes_%d" % m, align_bytes=64)
+            plane = keep.tile([P, P], U8, name="y_plane_%d" % m, align_bytes=64)
+            nc.vector.quantize_mx(out=codes[:].bitcast(FP8X4), scales=plane[:], in_=grouped[:].rearrange("s q t -> s (q t)"))
+            y_mx.append((codes, plane))
+
+        out_rows = out[0].rearrange("(m q) e -> q m e", q=P)
+        for j in range(E_TILES):
+            listed_v = keep.tile([P, N], BF16, name="listed_v_%d" % j)
+            nc.vector.tensor_copy(listed_v[:], v_pools[j][:].indirect(offsets[:]))
+            pairs = listed_v[:].bitcast(F32)
+            turned = psum.tile([P, PACK, P], F32, name="turned", bufs=2)
+            for u in range(2):
+                nc.tensor.transpose(turned[:, u, :], pairs[:, u : N // 2 : 2], identity[:])
+            grouped = ring.tile([P, P * PACK], BF16, name="v_grouped", align_bytes=64)
+            nc.scalar.copy(
+                grouped[:].bitcast(F32).rearrange("s (e u) -> s e u", u=2),
+                turned[:, 0:2, :].rearrange("s u e -> s e u"),
+            )
+            v_codes = keep.tile([P, P], U32, name="v_codes_%d" % j, align_bytes=64)
+            v_plane = keep.tile([P, P], U8, name="v_plane_%d" % j, align_bytes=64)
+            nc.vector.quantize_mx(out=v_codes[:].bitcast(FP8X4), scales=v_plane[:], in_=grouped[:])
+            sums = psum.tile([P, Q_TILES, P], F32, name="sums", bufs=2)
+            for m in range(Q_TILES):
+                codes, plane = y_mx[m]
+                nc.tensor.matmul_mx(
+                    out=sums[:, m, :],
+                    lhsT=codes[:].bitcast(FP8X4),
+                    lhsT_scale=plane[:],
+                    rhs=v_codes[:].bitcast(FP8X4),
+                    rhs_scale=v_plane[:],
+                    start=True,
+                    stop=True,
+                )
+            staged = keep.tile([P, Q_TILES, P], F32, name="staged_%d" % j)
+            nc.scalar.copy(staged[:], sums[:])
+            nc.sync.dma_start(out_rows[:, :, j * P : (j + 1) * P], staged[:])

@@ -23,6 +23,21 @@ Q_HALF = NQ // Q_HALVES
 Q_TILES = NQ // P
 E_TILES = DV // P
 SHIFT = 16
+SLOT = 4 * T
+LISTED = 4 * N
+EDGE = 64
+GROUPED = 2 * PACK * P
+CODES = 4 * P
+AT_K_WORDS = 0
+AT_Q = (0, SLOT)
+AT_K_BYTES = 2 * SLOT - T
+AT_C_PLANE = 2 * SLOT
+AT_C_WORDS = AT_C_PLANE + N
+AT_K_LISTED = AT_C_WORDS + SLOT
+AT_C_LISTED = AT_K_LISTED + LISTED
+AT_Q_WORK = AT_C_LISTED + LISTED
+AT_C_BYTES = AT_Q_WORK + 2 * GROUPED + 2 * CODES
+AT_V = (AT_C_BYTES, 0, SLOT, AT_C_BYTES)
 
 FLOPS = 2 * N * NQ * (2 * D + DV)
 
@@ -32,6 +47,7 @@ def tile_attend_at_resid_topk_kernel(tc, qT, k_words, k_scales, c_words, c_scale
     with ExitStack() as ctx:
         keep = ctx.enter_context(tc.tile_pool(name="keep", bufs=1))
         ring = ctx.enter_context(tc.tile_pool(name="ring", bufs=2))
+        stage = ctx.enter_context(tc.tile_pool(name="stage", bufs=1))
         psum = ctx.enter_context(tc.psum_pool(name="psum", bufs=1))
 
         offsets = keep.tile([P, N // 16], U16, name="offsets")
@@ -39,106 +55,125 @@ def tile_attend_at_resid_topk_kernel(tc, qT, k_words, k_scales, c_words, c_scale
 
         tables = (("k", k_words, k_scales), ("c", c_words, c_scales))
 
-        q_raw = []
-        for o in range(PASSES):
-            raw = keep.tile([P, PACK, NQ], F32, name="q_raw_%d" % o, tag="stage_%d" % o)
+        def load_queries(o, slot):
+            raw = stage.tile([P, PACK, NQ], F32, name="q_raw_%d" % o, offset=slot)
             rows = qT[0, o * P * PACK : (o + 1) * P * PACK, :]
             nc.sync.dma_start(raw[:], rows.rearrange("(p j) c -> p j c", j=PACK))
-            q_raw.append(raw)
+            return raw
 
-        byte_pools = []
-        for i, (name, words, scales) in enumerate(tables):
-            pool_bytes = keep.tile([P, T], U8, name=name + "_pool_bytes", tag="stage_%d" % (PASSES + i))
-            (nc.vector, nc.gpsimd)[i].memset(pool_bytes[:].bitcast(I32), 0)
+        def load_bytes(name, scales, slot, below, above):
+            wide = stage.tile([P, below + T + above], U8, name=name + "_pool_bytes", offset=slot - below)
+            pool_bytes = wide[:, below : below + T]
+            nc.vector.memset(pool_bytes.bitcast(I32), 0)
             rows = scales.rearrange("o (a r) t -> r a o t", r=4)
             for r in range(4):
-                queue = nc.gpsimd if (i == 1 and r >= 2) else nc.scalar
-                queue.dma_start(pool_bytes[r:P:SHIFT, :].bitcast(I32), rows[r].bitcast(I32))
-            byte_pools.append(pool_bytes)
+                nc.sync.dma_start(pool_bytes[r:P:SHIFT, :].bitcast(I32), rows[r].bitcast(I32))
+            return pool_bytes
+
+        def load_words(name, words, slot):
+            pool_words = stage.tile([P, T], I32, name=name + "_pool_words", offset=slot)
+            nc.sync.dma_start(pool_words[:], words[0].rearrange("p t b -> p (t b)").bitcast(I32))
+            return pool_words
+
+        ls_wide = stage.tile([Q_TILES, (LISTED + 2 * EDGE) // 4], F32, name="ls_wide", offset=AT_K_LISTED - EDGE)
+        ls_rows = ls_wide[:, 0:P]
+        nc.sync.dma_start(ls_rows, ls[0, 0].rearrange("(m p) -> m p", p=P))
+
+        word_pools = [load_words("k", k_words, AT_K_WORDS)]
+        byte_pools = [load_bytes("k", k_scales, AT_K_BYTES, 0, N)]
+
+        neg_rows = keep.tile([P, P], F32, name="neg_rows")
+        nc.vector.memset(neg_rows[:], 0.0)
+        nc.vector.tensor_scalar_mul(neg_rows[0:Q_TILES, :], ls_rows, -1.0)
+
+        word_pools.append(load_words("c", c_words, AT_C_WORDS))
+        byte_pools.append(load_bytes("c", c_scales, AT_C_BYTES, AT_C_BYTES - AT_C_LISTED, 0))
 
         identity = keep.tile([P, P], F32, name="identity")
         make_identity(nc, identity[:])
 
-        ls_cols = keep.tile([P, Q_TILES], F32, name="ls_cols")
-        with nc.allow_non_contiguous_dma(reason="one log-sum-exp a partition"):
-            nc.gpsimd.dma_start(ls_cols[:], ls[0, 0].rearrange("(m p) -> p m", p=P))
         us_cols = keep.tile([P, PACK], F32, name="us_cols")
-        nc.gpsimd.dma_start(us_cols[:], us[0].rearrange("(p t) one -> p (t one)", t=PACK))
+        nc.scalar.dma_start(us_cols[:], us[0].rearrange("(p t) one -> p (t one)", t=PACK))
+        ls_turned = psum.tile([P, PACK, P], F32, name="turned_v", bufs=2)
+        nc.tensor.transpose(ls_turned[:, 0, :], neg_rows[:], identity[:])
         neg_ls = keep.tile([P, Q_TILES], F32, name="neg_ls")
-        nc.gpsimd.tensor_scalar_mul(neg_ls[:], ls_cols[:], -1.0)
+        nc.scalar.copy(neg_ls[:], ls_turned[:, 0, 0:Q_TILES])
 
-        key_planes = []
-        for (name, words, scales), pool_bytes in zip(tables, byte_pools):
-            listed_bytes = keep.tile([P, N], U8, name=name + "_listed_bytes", align_bytes=64)
-            nc.vector.tensor_copy(listed_bytes[:], pool_bytes[:].indirect(offsets[:]))
+        def gather_words(name, pool_words, at):
+            listed_words = stage.tile([P, N], U32, name=name + "_listed_words", offset=at)
+            nc.vector.tensor_copy(listed_words[:], pool_words[:].bitcast(U32).indirect(offsets[:]))
+            return listed_words
+
+        def shift_plane(name, listed_bytes):
             moved_bytes = keep.tile([P, N], U8, name=name + "_moved_bytes", align_bytes=64)
             nc.vector.memset(moved_bytes[:].bitcast(I32), 0)
             nc.sync.dma_start(moved_bytes[0 : P - SHIFT, :].bitcast(I32), listed_bytes[SHIFT:P, :].bitcast(I32))
-            key_planes.append((listed_bytes, moved_bytes))
+            return (listed_bytes, moved_bytes)
 
-        word_pools = []
-        for i, (name, words, scales) in enumerate(tables):
-            pool_words = keep.tile([P, T], I32, name=name + "_pool_words", tag="stage_%d" % (PASSES + i))
-            nc.sync.dma_start(pool_words[:], words[0].rearrange("p t b -> p (t b)").bitcast(I32))
-            word_pools.append(pool_words)
-
-        q_mx = {}
-        for o in range(PASSES):
-            for h in range(Q_HALVES):
-                grouped = keep.tile([P, Q_HALF, PACK], BF16, name="q_grouped_%d_%d" % (h, o), align_bytes=64)
-                part = q_raw[o][:, :, h * Q_HALF : (h + 1) * Q_HALF].rearrange("p j c -> p c j")
-                if o == 0:
-                    nc.vector.tensor_copy(grouped[:], part)
-                else:
-                    nc.scalar.copy(grouped[:], part)
-                codes = keep.tile([P, Q_HALF], U32, name="q_codes_%d_%d" % (h, o), align_bytes=64)
-                plane = keep.tile([P, Q_HALF], U8, name="q_plane_%d_%d" % (h, o), align_bytes=64)
-                nc.vector.quantize_mx(out=codes[:].bitcast(FP8X4), scales=plane[:], in_=grouped[:].rearrange("p c j -> p (c j)"))
-                q_mx[h, o] = (codes, plane)
-
-        key_codes = []
-        for (name, words, scales), pool_words in zip(tables, word_pools):
-            listed_words = keep.tile([P, N], U32, name=name + "_listed_words", align_bytes=64)
-            nc.vector.tensor_copy(listed_words[:], pool_words[:].bitcast(U32).indirect(offsets[:]))
+        def part_words(name, listed_words):
             halves = keep.tile([P, PASSES, N], U16, name=name + "_halves", align_bytes=64)
             nc.vector.tensor_copy(halves[:], listed_words[:].bitcast(U16).rearrange("p (n o) -> p o n", o=PASSES))
-            key_codes.append(halves)
+            return halves
 
-        v_pools = []
-        for j in range(E_TILES):
-            v_pool = keep.tile([P, T], F32, name="v_pool_%d" % j, tag="stage_%d" % j)
-            nc.sync.dma_start(v_pool[:], vT[j * P : (j + 1) * P, :])
-            v_pools.append(v_pool)
+        k_listed = gather_words("k", word_pools[0], AT_K_LISTED)
+        k_plane = keep.tile([P, N], U8, name="k_plane", align_bytes=64)
+        nc.vector.tensor_copy(k_plane[:], byte_pools[0].indirect(offsets[:]))
+        q_raw = [load_queries(g, AT_Q[g]) for g in range(PASSES)]
+        key_planes = [shift_plane("k", k_plane)]
+        c_plane = stage.tile([P, N], U8, name="c_plane", offset=AT_C_PLANE, align_bytes=64)
+        nc.vector.tensor_copy(c_plane[:], byte_pools[1].indirect(offsets[:]))
+        key_planes.append(shift_plane("c", c_plane))
+        key_codes = [part_words("k", k_listed)]
+        key_codes.append(part_words("c", gather_words("c", word_pools[1], AT_C_LISTED)))
 
-        banks = [psum.tile([P, N], F32, name="scores_%d" % m) for m in range(Q_TILES)]
-
-        def score_pass(m, table, o):
-            h, cols = divmod(m * P, Q_HALF)
-            codes, plane = q_mx[h, o]
-            nc.tensor.matmul_mx(
-                out=banks[m][:],
-                lhsT=codes[:, cols : cols + P].bitcast(FP8X4),
-                lhsT_scale=plane[:, cols : cols + P],
-                rhs=key_codes[table][:, o, :].bitcast(FP4X4),
-                rhs_scale=key_planes[table][o][:],
-                start=(table == 0 and o == 0),
-                stop=(table == len(tables) - 1 and o == PASSES - 1),
-            )
+        banks = [psum.tile([P, N], F32, name="scores_%d" % m, tag="scores_%d" % m) for m in range(Q_TILES)]
 
         for o in range(PASSES):
             for m in range(Q_TILES):
-                score_pass(m, 0, o)
+                last = o == PASSES - 1 and m == Q_TILES - 1
+                if o == 0 and m % 2 == 1:
+                    grouped = stage.tile([P, P, PACK], BF16, name="q_grouped_0_%d" % m, offset=AT_Q_WORK + m // 2 * GROUPED, align_bytes=64)
+                else:
+                    grouped = keep.tile([P, P, PACK], BF16, name="q_grouped", tag="words_0" if last else "q_grouped_%d_%d" % (o, m), align_bytes=64)
+                part = q_raw[o][:, :, m * P : (m + 1) * P].rearrange("p j c -> p c j")
+                if (m + o) % 2 == 1:
+                    nc.vector.tensor_copy(grouped[:], part)
+                else:
+                    nc.scalar.copy(grouped[:], part)
+                if o == 0 and m % 2 == 0:
+                    codes = stage.tile([P, P], U32, name="q_codes_0_%d" % m, offset=AT_Q_WORK + 2 * GROUPED + m // 2 * CODES, align_bytes=64)
+                else:
+                    codes = keep.tile([P, P], U32, name="q_codes_%d_%d" % (o, m), align_bytes=64)
+                plane = keep.tile([P, P], U8, name="q_plane_%d_%d" % (o, m), align_bytes=64)
+                nc.vector.quantize_mx(out=codes[:].bitcast(FP8X4), scales=plane[:], in_=grouped[:].rearrange("p c j -> p (c j)"))
+                for table in range(2):
+                    nc.tensor.matmul_mx(
+                        out=banks[m][:],
+                        lhsT=codes[:].bitcast(FP8X4),
+                        lhsT_scale=plane[:],
+                        rhs=key_codes[table][:, o, :].bitcast(FP4X4),
+                        rhs_scale=key_planes[table][o][:],
+                        start=(table == 0 and o == 0),
+                        stop=(table == 1 and o == PASSES - 1),
+                    )
+
+        def load_values(j, slot):
+            v_pool = stage.tile([P, T], F32, name="v_pool_%d" % j, offset=slot)
+            nc.sync.dma_start(v_pool[:], vT[j * P : (j + 1) * P, :])
+            return v_pool
+
+        v_pools = [load_values(j, AT_V[j]) for j in range(E_TILES - 1)]
 
         y_mx = []
-        for m in range(Q_TILES):
-            for o in range(PASSES):
-                score_pass(m, 1, o)
+        v_mx = []
+
+        def weights_of(m, tag):
             dealt = ring.tile([P, PACK, P], F32, name="dealt")
             nc.scalar.activation(dealt[:], banks[m][:].rearrange("q (s t) -> q t s", t=PACK), EXP, bias=neg_ls[:, m : m + 1])
             turned = psum.tile([P, PACK, P], F32, name="turned", bufs=2)
             for t in range(PACK):
                 nc.tensor.transpose(turned[:, t, :], dealt[:, t, :], identity[:])
-            grouped = ring.tile([P, P, PACK], BF16, name="y_grouped", align_bytes=64)
+            grouped = keep.tile([P, P, PACK], BF16, name="y_grouped", tag=tag, align_bytes=64)
             nc.vector.tensor_tensor(
                 grouped[:],
                 turned[:].rearrange("s t q -> s q t"),
@@ -150,15 +185,14 @@ def tile_attend_at_resid_topk_kernel(tc, qT, k_words, k_scales, c_words, c_scale
             nc.vector.quantize_mx(out=codes[:].bitcast(FP8X4), scales=plane[:], in_=grouped[:].rearrange("s q t -> s (q t)"))
             y_mx.append((codes, plane))
 
-        out_rows = out[0].rearrange("(m q) e -> q m e", q=P)
-        for j in range(E_TILES):
-            listed_v = keep.tile([P, N], BF16, name="listed_v_%d" % j)
+        def values_of(j, tag):
+            listed_v = keep.tile([P, N], BF16, name="listed_v", tag=tag, align_bytes=64)
             nc.vector.tensor_copy(listed_v[:], v_pools[j][:].indirect(offsets[:]))
             pairs = listed_v[:].bitcast(F32)
-            turned = psum.tile([P, PACK, P], F32, name="turned", bufs=2)
+            turned = psum.tile([P, PACK, P], F32, name="turned_v", bufs=2)
             for u in range(2):
                 nc.tensor.transpose(turned[:, u, :], pairs[:, u : N // 2 : 2], identity[:])
-            grouped = ring.tile([P, P * PACK], BF16, name="v_grouped", align_bytes=64)
+            grouped = keep.tile([P, P * PACK], BF16, name="v_grouped", tag="v_grouped_%d" % j, align_bytes=64)
             nc.scalar.copy(
                 grouped[:].bitcast(F32).rearrange("s (e u) -> s e u", u=2),
                 turned[:, 0:2, :].rearrange("s u e -> s e u"),
@@ -166,7 +200,23 @@ def tile_attend_at_resid_topk_kernel(tc, qT, k_words, k_scales, c_words, c_scale
             v_codes = keep.tile([P, P], U32, name="v_codes_%d" % j, align_bytes=64)
             v_plane = keep.tile([P, P], U8, name="v_plane_%d" % j, align_bytes=64)
             nc.vector.quantize_mx(out=v_codes[:].bitcast(FP8X4), scales=v_plane[:], in_=grouped[:])
-            sums = psum.tile([P, Q_TILES, P], F32, name="sums", bufs=2)
+            v_mx.append((v_codes, v_plane))
+
+        values_of(0, "words_0")
+        v_pools.append(load_values(3, AT_V[3]))
+        weights_of(0, "words_1")
+        values_of(1, "words_1")
+        weights_of(1, "words_a")
+        weights_of(2, "words_2")
+        values_of(2, "words_2")
+        weights_of(3, "words_3")
+        values_of(3, "words_3")
+
+
+        out_rows = out[0].rearrange("(m q) e -> q m e", q=P)
+        for j in range(E_TILES):
+            v_codes, v_plane = v_mx[j]
+            sums = psum.tile([P, Q_TILES, P], F32, name="sums_%d" % j, tag="scores_%d" % j)
             for m in range(Q_TILES):
                 codes, plane = y_mx[m]
                 nc.tensor.matmul_mx(

@@ -13,13 +13,12 @@ FP8X4 = mybir.dt.float8_e4m3fn_x4
 FP4X4 = mybir.dt.float4_e2m1fn_x4
 EXP = mybir.ActivationFunctionType.Exp
 MULT = mybir.AluOpType.mult
+SUBTRACT = mybir.AluOpType.subtract
 
 P = 128
 PACK = 4
 N, T, D, NQ, DV = 512, 2048, 1024, 512, 512
 PASSES = D // (P * PACK)
-Q_HALVES = 2
-Q_HALF = NQ // Q_HALVES
 Q_TILES = NQ // P
 E_TILES = DV // P
 SHIFT = 16
@@ -28,16 +27,21 @@ LISTED = 4 * N
 EDGE = 64
 GROUPED = 2 * PACK * P
 CODES = 4 * P
+PITCH = SLOT + CODES
 AT_K_WORDS = 0
-AT_Q = (0, SLOT)
-AT_K_BYTES = 2 * SLOT - T
-AT_C_PLANE = 2 * SLOT
-AT_C_WORDS = AT_C_PLANE + N
-AT_K_LISTED = AT_C_WORDS + SLOT
-AT_C_LISTED = AT_K_LISTED + LISTED
-AT_Q_WORK = AT_C_LISTED + LISTED
-AT_C_BYTES = AT_Q_WORK + 2 * GROUPED + 2 * CODES
-AT_V = (AT_C_BYTES, 0, SLOT, AT_C_BYTES)
+AT_K_BYTES = AT_K_WORDS + SLOT
+AT_C_PLANE = AT_K_BYTES + T
+AT_Q_GROUPED = AT_C_PLANE + N
+AT_C_LISTED = AT_Q_GROUPED + Q_TILES * GROUPED - EDGE
+AT_Q_CODES = AT_C_LISTED + LISTED
+AT_V = AT_Q_CODES + Q_TILES * CODES
+AT_LS = AT_V + E_TILES * PITCH
+AT_Q0 = AT_LS + 4 * P
+AT_K_LISTED = AT_Q0 + SLOT
+AT_C_WORDS = AT_K_LISTED + LISTED
+AT_Q1 = AT_C_WORDS + SLOT
+AT_Y_LATE = AT_Q1 + SLOT
+AT_V_SECOND = AT_Y_LATE + 2 * GROUPED
 
 FLOPS = 2 * N * NQ * (2 * D + DV)
 
@@ -52,8 +56,6 @@ def tile_attend_at_resid_topk_kernel(tc, qT, k_words, k_scales, c_words, c_scale
 
         offsets = keep.tile([P, N // 16], U16, name="offsets")
         nc.sync.dma_start(offsets[:], offs)
-
-        tables = (("k", k_words, k_scales), ("c", c_words, c_scales))
 
         def load_queries(o, slot):
             raw = stage.tile([P, PACK, NQ], F32, name="q_raw_%d" % o, offset=slot)
@@ -75,29 +77,29 @@ def tile_attend_at_resid_topk_kernel(tc, qT, k_words, k_scales, c_words, c_scale
             nc.sync.dma_start(pool_words[:], words[0].rearrange("p t b -> p (t b)").bitcast(I32))
             return pool_words
 
-        ls_wide = stage.tile([Q_TILES, (LISTED + 2 * EDGE) // 4], F32, name="ls_wide", offset=AT_K_LISTED - EDGE)
+        ls_wide = stage.tile([Q_TILES, P + EDGE // 4], F32, name="ls_wide", offset=AT_LS)
         ls_rows = ls_wide[:, 0:P]
         nc.sync.dma_start(ls_rows, ls[0, 0].rearrange("(m p) -> m p", p=P))
 
         word_pools = [load_words("k", k_words, AT_K_WORDS)]
         byte_pools = [load_bytes("k", k_scales, AT_K_BYTES, 0, N)]
 
-        neg_rows = keep.tile([P, P], F32, name="neg_rows")
-        nc.vector.memset(neg_rows[:], 0.0)
-        nc.vector.tensor_scalar_mul(neg_rows[0:Q_TILES, :], ls_rows, -1.0)
+        padded = stage.tile([P, (SLOT + 2 * EDGE) // 4], F32, name="padded", offset=AT_C_WORDS - EDGE)
+        nc.vector.memset(padded[:, 0 : P + Q_TILES], 0.0)
+        nc.vector.tensor_copy(padded[0:Q_TILES, 0:P], ls_rows)
 
-        word_pools.append(load_words("c", c_words, AT_C_WORDS))
-        byte_pools.append(load_bytes("c", c_scales, AT_C_BYTES, AT_C_BYTES - AT_C_LISTED, 0))
+        q_raw = [load_queries(0, AT_Q0)]
+        byte_pools.append(load_bytes("c", c_scales, AT_V, AT_V - AT_Q_CODES + EDGE, AT_LS - AT_V - T + EDGE))
 
         identity = keep.tile([P, P], F32, name="identity")
         make_identity(nc, identity[:])
 
         us_cols = keep.tile([P, PACK], F32, name="us_cols")
         nc.scalar.dma_start(us_cols[:], us[0].rearrange("(p t) one -> p (t one)", t=PACK))
-        ls_turned = psum.tile([P, PACK, P], F32, name="turned_v", bufs=2)
-        nc.tensor.transpose(ls_turned[:, 0, :], neg_rows[:], identity[:])
+        ls_turned = psum.tile([P, PACK, P], F32, name="turned", bufs=4)
+        nc.tensor.transpose(ls_turned[:, 0, :], padded[:, 0:P], identity[:])
         neg_ls = keep.tile([P, Q_TILES], F32, name="neg_ls")
-        nc.scalar.copy(neg_ls[:], ls_turned[:, 0, 0:Q_TILES])
+        nc.vector.tensor_tensor(neg_ls[:], padded[:, P : P + Q_TILES], ls_turned[:, 0, 0:Q_TILES], SUBTRACT)
 
         def gather_words(name, pool_words, at):
             listed_words = stage.tile([P, N], U32, name=name + "_listed_words", offset=at)
@@ -118,116 +120,164 @@ def tile_attend_at_resid_topk_kernel(tc, qT, k_words, k_scales, c_words, c_scale
         k_listed = gather_words("k", word_pools[0], AT_K_LISTED)
         k_plane = keep.tile([P, N], U8, name="k_plane", align_bytes=64)
         nc.vector.tensor_copy(k_plane[:], byte_pools[0].indirect(offsets[:]))
-        q_raw = [load_queries(g, AT_Q[g]) for g in range(PASSES)]
+        word_pools.append(load_words("c", c_words, AT_C_WORDS))
+        q_raw.append(load_queries(1, AT_Q1))
         key_planes = [shift_plane("k", k_plane)]
         c_plane = stage.tile([P, N], U8, name="c_plane", offset=AT_C_PLANE, align_bytes=64)
         nc.vector.tensor_copy(c_plane[:], byte_pools[1].indirect(offsets[:]))
         key_planes.append(shift_plane("c", c_plane))
         key_codes = [part_words("k", k_listed)]
-        key_codes.append(part_words("c", gather_words("c", word_pools[1], AT_C_LISTED)))
 
         banks = [psum.tile([P, N], F32, name="scores_%d" % m, tag="scores_%d" % m) for m in range(Q_TILES)]
 
-        for o in range(PASSES):
-            for m in range(Q_TILES):
-                last = o == PASSES - 1 and m == Q_TILES - 1
-                if o == 0 and m % 2 == 1:
-                    grouped = stage.tile([P, P, PACK], BF16, name="q_grouped_0_%d" % m, offset=AT_Q_WORK + m // 2 * GROUPED, align_bytes=64)
-                else:
-                    grouped = keep.tile([P, P, PACK], BF16, name="q_grouped", tag="words_0" if last else "q_grouped_%d_%d" % (o, m), align_bytes=64)
-                part = q_raw[o][:, :, m * P : (m + 1) * P].rearrange("p j c -> p c j")
-                if (m + o) % 2 == 1:
-                    nc.vector.tensor_copy(grouped[:], part)
-                else:
-                    nc.scalar.copy(grouped[:], part)
-                if o == 0 and m % 2 == 0:
-                    codes = stage.tile([P, P], U32, name="q_codes_0_%d" % m, offset=AT_Q_WORK + 2 * GROUPED + m // 2 * CODES, align_bytes=64)
-                else:
-                    codes = keep.tile([P, P], U32, name="q_codes_%d_%d" % (o, m), align_bytes=64)
-                plane = keep.tile([P, P], U8, name="q_plane_%d_%d" % (o, m), align_bytes=64)
-                nc.vector.quantize_mx(out=codes[:].bitcast(FP8X4), scales=plane[:], in_=grouped[:].rearrange("p c j -> p (c j)"))
-                for table in range(2):
-                    nc.tensor.matmul_mx(
-                        out=banks[m][:],
-                        lhsT=codes[:].bitcast(FP8X4),
-                        lhsT_scale=plane[:],
-                        rhs=key_codes[table][:, o, :].bitcast(FP4X4),
-                        rhs_scale=key_planes[table][o][:],
-                        start=(table == 0 and o == 0),
-                        stop=(table == 1 and o == PASSES - 1),
-                    )
+        def quantise_queries(o, m, grouped):
+            part = q_raw[o][:, :, m * P : (m + 1) * P].rearrange("p j c -> p c j")
+            if o == 1 and m % 2 == 0:
+                nc.vector.tensor_copy(grouped[:, m], part)
+            else:
+                nc.scalar.copy(grouped[:, m], part)
+            if o == 0:
+                codes = stage.tile([P, P], U32, name="q_codes_0_%d" % m, offset=AT_Q_CODES + m * CODES, align_bytes=64)
+            else:
+                codes = keep.tile([P, P], U32, name="q_codes_1_%d" % m, align_bytes=64)
+            plane = keep.tile([P, P], U8, name="q_plane_%d_%d" % (o, m), align_bytes=64)
+            nc.vector.quantize_mx(out=codes[:].bitcast(FP8X4), scales=plane[:], in_=grouped[:, m].rearrange("p c j -> p (c j)"))
+            return codes, plane
+
+        def grouped_queries(o):
+            return stage.tile([P, Q_TILES, P, PACK], BF16, name="q_grouped_%d" % o, offset=AT_Q_GROUPED, align_bytes=64)
+
+        def score_pass(q_mx, m, table, o):
+            codes, plane = q_mx
+            nc.tensor.matmul_mx(
+                out=banks[m][:],
+                lhsT=codes[:].bitcast(FP8X4),
+                lhsT_scale=plane[:],
+                rhs=key_codes[table][:, o, :].bitcast(FP4X4),
+                rhs_scale=key_planes[table][o][:],
+                start=(table == 0 and o == 0),
+                stop=(table == 1 and o == PASSES - 1),
+            )
+
+        q_first = []
+        q_grouped = grouped_queries(0)
+        for m in range(Q_TILES):
+            q_first.append(quantise_queries(0, m, q_grouped))
+            score_pass(q_first[m], m, 0, 0)
+        key_codes.append(part_words("c", gather_words("c", word_pools[1], AT_C_LISTED)))
+        for m in range(Q_TILES):
+            score_pass(q_first[m], m, 1, 0)
+        q_grouped = grouped_queries(1)
+        for m in range(Q_TILES):
+            q_second = quantise_queries(1, m, q_grouped)
+            for table in range(2):
+                score_pass(q_second, m, table, 1)
 
         def load_values(j, slot):
             v_pool = stage.tile([P, T], F32, name="v_pool_%d" % j, offset=slot)
             nc.sync.dma_start(v_pool[:], vT[j * P : (j + 1) * P, :])
             return v_pool
 
-        v_pools = [load_values(j, AT_V[j]) for j in range(E_TILES - 1)]
+        v_pools = [load_values(j, AT_V + j * PITCH) for j in range(E_TILES)]
 
         y_mx = []
-        v_mx = []
 
-        def weights_of(m, tag):
-            dealt = ring.tile([P, PACK, P], F32, name="dealt")
-            nc.scalar.activation(dealt[:], banks[m][:].rearrange("q (s t) -> q t s", t=PACK), EXP, bias=neg_ls[:, m : m + 1])
-            turned = psum.tile([P, PACK, P], F32, name="turned", bufs=2)
-            for t in range(PACK):
-                nc.tensor.transpose(turned[:, t, :], dealt[:, t, :], identity[:])
-            grouped = keep.tile([P, P, PACK], BF16, name="y_grouped", tag=tag, align_bytes=64)
-            nc.vector.tensor_tensor(
-                grouped[:],
-                turned[:].rearrange("s t q -> s q t"),
-                us_cols[:].unsqueeze(1).to_broadcast([P, P, PACK]),
-                MULT,
-            )
-            codes = keep.tile([P, P], U32, name="y_codes_%d" % m, align_bytes=64)
-            plane = keep.tile([P, P], U8, name="y_plane_%d" % m, align_bytes=64)
-            nc.vector.quantize_mx(out=codes[:].bitcast(FP8X4), scales=plane[:], in_=grouped[:].rearrange("s q t -> s (q t)"))
-            y_mx.append((codes, plane))
+        def weights_of(pair, grouped):
+            for i in range(2):
+                m = 2 * pair + i
+                dealt = ring.tile([P, PACK, P], F32, name="dealt")
+                nc.scalar.activation(dealt[:], banks[m][:].rearrange("q (s t) -> q t s", t=PACK), EXP, bias=neg_ls[:, m : m + 1])
+                turned = psum.tile([P, PACK, P], F32, name="turned", bufs=4)
+                for t in range(PACK):
+                    nc.tensor.transpose(turned[:, t, :], dealt[:, t, :], identity[:])
+                nc.vector.tensor_tensor(
+                    grouped[:, i],
+                    turned[:].rearrange("s t q -> s q t"),
+                    us_cols[:].unsqueeze(1).to_broadcast([P, P, PACK]),
+                    MULT,
+                )
+            codes = keep.tile([P, 2 * P], U32, name="y_codes_%d" % pair, align_bytes=64)
+            plane = keep.tile([P, 2 * P], U8, name="y_plane_%d" % pair, align_bytes=64)
+            nc.vector.quantize_mx(out=codes[:].bitcast(FP8X4), scales=plane[:], in_=grouped[:].rearrange("s i q t -> s (i q t)"))
+            for i in range(2):
+                y_mx.append((codes[:, i * P : (i + 1) * P], plane[:, i * P : (i + 1) * P]))
 
-        def values_of(j, tag):
-            listed_v = keep.tile([P, N], BF16, name="listed_v", tag=tag, align_bytes=64)
+        def gather_values(j, at):
+            listed_v = stage.tile([P, N], BF16, name="listed_v_%d" % j, offset=at)
             nc.vector.tensor_copy(listed_v[:], v_pools[j][:].indirect(offsets[:]))
+            return listed_v
+
+        def turn_values(listed_v, grouped):
             pairs = listed_v[:].bitcast(F32)
-            turned = psum.tile([P, PACK, P], F32, name="turned_v", bufs=2)
+            turned = psum.tile([P, PACK, P], F32, name="turned", bufs=4)
             for u in range(2):
                 nc.tensor.transpose(turned[:, u, :], pairs[:, u : N // 2 : 2], identity[:])
-            grouped = keep.tile([P, P * PACK], BF16, name="v_grouped", tag="v_grouped_%d" % j, align_bytes=64)
             nc.scalar.copy(
                 grouped[:].bitcast(F32).rearrange("s (e u) -> s e u", u=2),
                 turned[:, 0:2, :].rearrange("s u e -> s e u"),
             )
-            v_codes = keep.tile([P, P], U32, name="v_codes_%d" % j, align_bytes=64)
-            v_plane = keep.tile([P, P], U8, name="v_plane_%d" % j, align_bytes=64)
-            nc.vector.quantize_mx(out=v_codes[:].bitcast(FP8X4), scales=v_plane[:], in_=grouped[:])
-            v_mx.append((v_codes, v_plane))
 
-        values_of(0, "words_0")
-        v_pools.append(load_values(3, AT_V[3]))
-        weights_of(0, "words_1")
-        values_of(1, "words_1")
-        weights_of(1, "words_a")
-        weights_of(2, "words_2")
-        values_of(2, "words_2")
-        weights_of(3, "words_3")
-        values_of(3, "words_3")
-
+        def quantise_values(j, grouped):
+            if 0 < j < E_TILES - 1:
+                at = AT_V + (j + 1) * PITCH + SLOT - EDGE
+                wide = stage.tile([P, (EDGE + CODES) // 4], U32, name="v_codes_%d" % j, offset=at, align_bytes=64)
+                codes = wide[:, EDGE // 4 :]
+            else:
+                whole = keep.tile([P, P], U32, name="v_codes_%d" % j, align_bytes=64)
+                codes = whole[:]
+            plane = keep.tile([P, P], U8, name="v_plane_%d" % j, align_bytes=64)
+            nc.vector.quantize_mx(out=codes.bitcast(FP8X4), scales=plane[:], in_=grouped[:])
+            return codes, plane
 
         out_rows = out[0].rearrange("(m q) e -> q m e", q=P)
-        for j in range(E_TILES):
-            v_codes, v_plane = v_mx[j]
-            sums = psum.tile([P, Q_TILES, P], F32, name="sums_%d" % j, tag="scores_%d" % j)
-            for m in range(Q_TILES):
-                codes, plane = y_mx[m]
+
+        def products(v_mx, sums, first, count):
+            v_codes, v_plane = v_mx
+            for i in range(count):
+                codes, plane = y_mx[first + i]
                 nc.tensor.matmul_mx(
-                    out=sums[:, m, :],
-                    lhsT=codes[:].bitcast(FP8X4),
-                    lhsT_scale=plane[:],
-                    rhs=v_codes[:].bitcast(FP8X4),
+                    out=sums[:, i, :],
+                    lhsT=codes.bitcast(FP8X4),
+                    lhsT_scale=plane,
+                    rhs=v_codes.bitcast(FP8X4),
                     rhs_scale=v_plane[:],
                     start=True,
                     stop=True,
                 )
+
+        def finish_values(j, grouped):
+            v_mx = quantise_values(j, grouped)
+            sums = psum.tile([P, Q_TILES, P], F32, name="sums_%d" % j, tag="scores_%d" % j)
+            products(v_mx, sums, 0, Q_TILES)
             staged = keep.tile([P, Q_TILES, P], F32, name="staged_%d" % j)
             nc.scalar.copy(staged[:], sums[:])
             nc.sync.dma_start(out_rows[:, :, j * P : (j + 1) * P], staged[:])
+
+        listed_v = gather_values(0, AT_Q_GROUPED)
+        y_early = keep.tile([P, 2, P, PACK], BF16, name="y_early", align_bytes=64)
+        weights_of(0, y_early)
+        y_late = stage.tile([P, 2, P, PACK], BF16, name="y_late", offset=AT_Y_LATE, align_bytes=64)
+        weights_of(1, y_late)
+
+        v_grouped = [keep.tile([P, N], BF16, name="v_grouped_%d" % j, align_bytes=64) for j in (0, 2, 3)]
+        v_grouped = [v_grouped[0], stage.tile([P, N], BF16, name="v_grouped_1", offset=AT_V_SECOND, align_bytes=64)] + v_grouped[1:]
+        turn_values(listed_v, v_grouped[0])
+        finish_values(0, v_grouped[0])
+        turn_values(gather_values(1, AT_Y_LATE), v_grouped[1])
+        turn_values(gather_values(2, AT_Y_LATE + GROUPED), v_grouped[2])
+        finish_values(1, v_grouped[1])
+        turn_values(gather_values(3, AT_V_SECOND), v_grouped[3])
+        finish_values(2, v_grouped[2])
+
+        j = E_TILES - 1
+        v_mx = quantise_values(j, v_grouped[j])
+        low = psum.tile([P, 2, P], F32, name="low", tag="scores_%d" % j)
+        products(v_mx, low, 0, 2)
+        high = psum.tile([P, 2, P], F32, name="high", tag="scores_0")
+        products(v_mx, high, 2, 2)
+        staged_low = keep.tile([P, 2, P], F32, name="staged_low")
+        nc.vector.tensor_copy(staged_low[:], low[:])
+        nc.sync.dma_start(out_rows[:, 0:2, j * P : (j + 1) * P], staged_low[:])
+        staged_high = keep.tile([P, 2, P], F32, name="staged_high")
+        nc.scalar.copy(staged_high[:], high[:])
+        nc.scalar.dma_start(out_rows[:, 2:4, j * P : (j + 1) * P], staged_high[:])

@@ -117,7 +117,7 @@ def tile_attend_at_resid_topk_kernel(tc, qT, k_words, k_scales, c_words, c_scale
             nc.vector.tensor_copy(halves[:], listed_words[:].bitcast(U16).rearrange("p (n o) -> p o n", o=PASSES))
             return halves
 
-        k_listed = gather_words("k", word_pools[0], AT_K_LISTED)
+        key_codes = [part_words("k", gather_words("k", word_pools[0], AT_K_LISTED))]
         k_plane = keep.tile([P, N], U8, name="k_plane", align_bytes=64)
         nc.vector.tensor_copy(k_plane[:], byte_pools[0].indirect(offsets[:]))
         word_pools.append(load_words("c", c_words, AT_C_WORDS))
@@ -126,7 +126,6 @@ def tile_attend_at_resid_topk_kernel(tc, qT, k_words, k_scales, c_words, c_scale
         c_plane = stage.tile([P, N], U8, name="c_plane", offset=AT_C_PLANE, align_bytes=64)
         nc.vector.tensor_copy(c_plane[:], byte_pools[1].indirect(offsets[:]))
         key_planes.append(shift_plane("c", c_plane))
-        key_codes = [part_words("k", k_listed)]
 
         banks = [psum.tile([P, N], F32, name="scores_%d" % m, tag="scores_%d" % m) for m in range(Q_TILES)]
 
@@ -159,6 +158,14 @@ def tile_attend_at_resid_topk_kernel(tc, qT, k_words, k_scales, c_words, c_scale
                 stop=(table == 1 and o == PASSES - 1),
             )
 
+        def turn_weights(m):
+            dealt = ring.tile([P, PACK, P], F32, name="dealt")
+            nc.scalar.activation(dealt[:], banks[m][:].rearrange("q (s t) -> q t s", t=PACK), EXP, bias=neg_ls[:, m : m + 1])
+            turned = psum.tile([P, PACK, P], F32, name="turned", bufs=4)
+            for t in range(PACK):
+                nc.tensor.transpose(turned[:, t, :], dealt[:, t, :], identity[:])
+            return turned
+
         q_first = []
         q_grouped = grouped_queries(0)
         for m in range(Q_TILES):
@@ -168,10 +175,12 @@ def tile_attend_at_resid_topk_kernel(tc, qT, k_words, k_scales, c_words, c_scale
         for m in range(Q_TILES):
             score_pass(q_first[m], m, 1, 0)
         q_grouped = grouped_queries(1)
+        y_turned = []
         for m in range(Q_TILES):
             q_second = quantise_queries(1, m, q_grouped)
             for table in range(2):
                 score_pass(q_second, m, table, 1)
+            y_turned.append(turn_weights(m))
 
         def load_values(j, slot):
             v_pool = stage.tile([P, T], F32, name="v_pool_%d" % j, offset=slot)
@@ -184,15 +193,9 @@ def tile_attend_at_resid_topk_kernel(tc, qT, k_words, k_scales, c_words, c_scale
 
         def weights_of(pair, grouped):
             for i in range(2):
-                m = 2 * pair + i
-                dealt = ring.tile([P, PACK, P], F32, name="dealt")
-                nc.scalar.activation(dealt[:], banks[m][:].rearrange("q (s t) -> q t s", t=PACK), EXP, bias=neg_ls[:, m : m + 1])
-                turned = psum.tile([P, PACK, P], F32, name="turned", bufs=4)
-                for t in range(PACK):
-                    nc.tensor.transpose(turned[:, t, :], dealt[:, t, :], identity[:])
                 nc.vector.tensor_tensor(
                     grouped[:, i],
-                    turned[:].rearrange("s t q -> s q t"),
+                    y_turned[2 * pair + i][:].rearrange("s t q -> s q t"),
                     us_cols[:].unsqueeze(1).to_broadcast([P, P, PACK]),
                     MULT,
                 )
@@ -254,7 +257,7 @@ def tile_attend_at_resid_topk_kernel(tc, qT, k_words, k_scales, c_words, c_scale
             nc.sync.dma_start(out_rows[:, :, j * P : (j + 1) * P], staged[:])
 
         listed_v = gather_values(0, AT_Q_GROUPED)
-        y_early = keep.tile([P, 2, P, PACK], BF16, name="y_early", align_bytes=64)
+        y_early = stage.tile([P, 2, P, PACK], BF16, name="y_early", offset=AT_V, align_bytes=64)
         weights_of(0, y_early)
         y_late = stage.tile([P, 2, P, PACK], BF16, name="y_late", offset=AT_Y_LATE, align_bytes=64)
         weights_of(1, y_late)

@@ -12,8 +12,8 @@ U8 = mybir.dt.uint8
 FP8X4 = mybir.dt.float8_e4m3fn_x4
 FP4X4 = mybir.dt.float4_e2m1fn_x4
 EXP = mybir.ActivationFunctionType.Exp
+COPY = mybir.ActivationFunctionType.Copy
 MULT = mybir.AluOpType.mult
-SUBTRACT = mybir.AluOpType.subtract
 
 P = 128
 PACK = 4
@@ -21,27 +21,11 @@ N, T, D, NQ, DV = 512, 2048, 1024, 512, 512
 PASSES = D // (P * PACK)
 Q_TILES = NQ // P
 E_TILES = DV // P
+LIST_COLS = N // 16
 SHIFT = 16
 SLOT = 4 * T
-LISTED = 4 * N
-EDGE = 64
-GROUPED = 2 * PACK * P
-CODES = 4 * P
-PITCH = SLOT + CODES
-AT_K_WORDS = 0
-AT_K_BYTES = AT_K_WORDS + SLOT
-AT_C_PLANE = AT_K_BYTES + T
-AT_Q_GROUPED = AT_C_PLANE + N
-AT_C_LISTED = AT_Q_GROUPED + Q_TILES * GROUPED - EDGE
-AT_Q_CODES = AT_C_LISTED + LISTED
-AT_V = AT_Q_CODES + Q_TILES * CODES
-AT_LS = AT_V + E_TILES * PITCH
-AT_Q0 = AT_LS + 4 * P
-AT_K_LISTED = AT_Q0 + SLOT
-AT_C_WORDS = AT_K_LISTED + LISTED
-AT_Q1 = AT_C_WORDS + SLOT
-AT_Y_LATE = AT_Q1 + SLOT
-AT_V_SECOND = AT_Y_LATE + 2 * GROUPED
+AT_K_BYTES = E_TILES * SLOT
+AT_C_BYTES = AT_K_BYTES + T
 
 FLOPS = 2 * N * NQ * (2 * D + DV)
 
@@ -54,97 +38,90 @@ def tile_attend_at_resid_topk_kernel(tc, qT, k_words, k_scales, c_words, c_scale
         stage = ctx.enter_context(tc.tile_pool(name="stage", bufs=1))
         psum = ctx.enter_context(tc.psum_pool(name="psum", bufs=1))
 
-        offsets = keep.tile([P, N // 16], U16, name="offsets")
+        offsets = keep.tile([P, LIST_COLS], U16, name="offsets")
         nc.sync.dma_start(offsets[:], offs)
 
-        def load_queries(o, slot):
-            raw = stage.tile([P, PACK, NQ], F32, name="q_raw_%d" % o, offset=slot)
-            rows = qT[0, o * P * PACK : (o + 1) * P * PACK, :]
-            nc.sync.dma_start(raw[:], rows.rearrange("(p j) c -> p j c", j=PACK))
-            return raw
+        def load_words(name, words):
+            pool_words = keep.tile([P, T], I32, name=name + "_pool_words")
+            nc.sync.dma_start(pool_words[:], words[0].rearrange("p t b -> p (t b)").bitcast(I32))
+            return pool_words
 
-        def load_bytes(name, scales, slot, below, above):
-            wide = stage.tile([P, below + T + above], U8, name=name + "_pool_bytes", offset=slot - below)
-            pool_bytes = wide[:, below : below + T]
-            nc.vector.memset(pool_bytes.bitcast(I32), 0)
+        def load_bytes(name, scales, engine, at):
+            pool_bytes = stage.tile([P, T], U8, name=name + "_pool_bytes", offset=at)
+            engine.memset(pool_bytes[:].bitcast(I32), 0)
             rows = scales.rearrange("o (a r) t -> r a o t", r=4)
             for r in range(4):
                 nc.sync.dma_start(pool_bytes[r:P:SHIFT, :].bitcast(I32), rows[r].bitcast(I32))
             return pool_bytes
 
-        def load_words(name, words, slot):
-            pool_words = stage.tile([P, T], I32, name=name + "_pool_words", offset=slot)
-            nc.sync.dma_start(pool_words[:], words[0].rearrange("p t b -> p (t b)").bitcast(I32))
-            return pool_words
+        def load_queries(o):
+            raw = keep.tile([P, PACK, NQ], F32, name="q_raw_%d" % o)
+            rows = qT[0, o * P * PACK : (o + 1) * P * PACK, :]
+            nc.sync.dma_start(raw[:], rows.rearrange("(p j) c -> p j c", j=PACK))
+            return raw
 
-        ls_wide = stage.tile([Q_TILES, P + EDGE // 4], F32, name="ls_wide", offset=AT_LS)
-        ls_rows = ls_wide[:, 0:P]
-        nc.sync.dma_start(ls_rows, ls[0, 0].rearrange("(m p) -> m p", p=P))
+        word_pools = [load_words("k", k_words)]
+        byte_pools = [load_bytes("k", k_scales, nc.gpsimd, AT_K_BYTES)]
+        q_raw = [load_queries(0)]
+        byte_pools.append(load_bytes("c", c_scales, nc.vector, AT_C_BYTES))
+        word_pools.append(load_words("c", c_words))
+        q_raw.append(load_queries(1))
 
-        word_pools = [load_words("k", k_words, AT_K_WORDS)]
-        byte_pools = [load_bytes("k", k_scales, AT_K_BYTES, 0, N)]
-
-        padded = stage.tile([P, (SLOT + 2 * EDGE) // 4], F32, name="padded", offset=AT_C_WORDS - EDGE)
-        nc.vector.memset(padded[:, 0 : P + Q_TILES], 0.0)
-        nc.vector.tensor_copy(padded[0:Q_TILES, 0:P], ls_rows)
-
-        q_raw = [load_queries(0, AT_Q0)]
-        byte_pools.append(load_bytes("c", c_scales, AT_V, AT_V - AT_Q_CODES + EDGE, AT_LS - AT_V - T + EDGE))
-
+        padded = keep.tile([P, P], F32, name="padded")
+        nc.gpsimd.memset(padded[:], 0.0)
+        nc.gpsimd.dma_start(padded[0:Q_TILES, :], ls[0, 0].rearrange("(m p) -> m p", p=P))
         identity = keep.tile([P, P], F32, name="identity")
         make_identity(nc, identity[:])
 
         us_cols = keep.tile([P, PACK], F32, name="us_cols")
-        nc.scalar.dma_start(us_cols[:], us[0].rearrange("(p t) one -> p (t one)", t=PACK))
+        nc.gpsimd.dma_start(us_cols[:], us[0].rearrange("(p t) one -> p (t one)", t=PACK))
         ls_turned = psum.tile([P, PACK, P], F32, name="turned", bufs=4)
-        nc.tensor.transpose(ls_turned[:, 0, :], padded[:, 0:P], identity[:])
+        nc.tensor.transpose(ls_turned[:, 0, :], padded[:], identity[:])
         neg_ls = keep.tile([P, Q_TILES], F32, name="neg_ls")
-        nc.vector.tensor_tensor(neg_ls[:], padded[:, P : P + Q_TILES], ls_turned[:, 0, 0:Q_TILES], SUBTRACT)
+        nc.scalar.activation(neg_ls[:], ls_turned[:, 0, 0:Q_TILES], COPY, scale=-1.0)
 
-        def gather_words(name, pool_words, at):
-            listed_words = stage.tile([P, N], U32, name=name + "_listed_words", offset=at)
+
+        def gather_words(name, pool_words):
+            listed_words = keep.tile([P, N], U32, name=name + "_listed_words")
             nc.vector.tensor_copy(listed_words[:], pool_words[:].bitcast(U32).indirect(offsets[:]))
-            return listed_words
+            halves = keep.tile([P, PASSES, N], U16, name=name + "_halves", align_bytes=64)
+            nc.vector.tensor_copy(halves[:], listed_words[:].bitcast(U16).rearrange("p (n o) -> p o n", o=PASSES))
+            return halves
 
-        def shift_plane(name, listed_bytes):
+        def gather_bytes(name, pool_bytes):
+            listed_bytes = keep.tile([P, N], U8, name=name + "_listed_bytes", align_bytes=64)
+            nc.vector.tensor_copy(listed_bytes[:], pool_bytes[:].indirect(offsets[:]))
             moved_bytes = keep.tile([P, N], U8, name=name + "_moved_bytes", align_bytes=64)
             nc.vector.memset(moved_bytes[:].bitcast(I32), 0)
             nc.sync.dma_start(moved_bytes[0 : P - SHIFT, :].bitcast(I32), listed_bytes[SHIFT:P, :].bitcast(I32))
             return (listed_bytes, moved_bytes)
 
-        def part_words(name, listed_words):
-            halves = keep.tile([P, PASSES, N], U16, name=name + "_halves", align_bytes=64)
-            nc.vector.tensor_copy(halves[:], listed_words[:].bitcast(U16).rearrange("p (n o) -> p o n", o=PASSES))
-            return halves
+        key_codes = [gather_words("k", word_pools[0])]
+        key_planes = [gather_bytes("k", byte_pools[0])]
+        key_planes.append(gather_bytes("c", byte_pools[1]))
 
-        key_codes = [part_words("k", gather_words("k", word_pools[0], AT_K_LISTED))]
-        k_plane = keep.tile([P, N], U8, name="k_plane", align_bytes=64)
-        nc.vector.tensor_copy(k_plane[:], byte_pools[0].indirect(offsets[:]))
-        word_pools.append(load_words("c", c_words, AT_C_WORDS))
-        q_raw.append(load_queries(1, AT_Q1))
-        key_planes = [shift_plane("k", k_plane)]
-        c_plane = stage.tile([P, N], U8, name="c_plane", offset=AT_C_PLANE, align_bytes=64)
-        nc.vector.tensor_copy(c_plane[:], byte_pools[1].indirect(offsets[:]))
-        key_planes.append(shift_plane("c", c_plane))
+        def load_values(j):
+            v_pool = stage.tile([P, T], F32, name="v_pool_%d" % j, offset=j * SLOT)
+            nc.sync.dma_start(v_pool[:], vT[j * P : (j + 1) * P, :])
+            return v_pool
 
+        v_pools = [load_values(j) for j in range(E_TILES)]
         banks = [psum.tile([P, N], F32, name="scores_%d" % m, tag="scores_%d" % m) for m in range(Q_TILES)]
 
-        def quantise_queries(o, m, grouped):
+        def quantise_queries(o, m):
+            grouped = keep.tile([P, P, PACK], BF16, name="q_grouped_%d_%d" % (o, m), align_bytes=64)
             part = q_raw[o][:, :, m * P : (m + 1) * P].rearrange("p j c -> p c j")
             if o == 1 and m % 2 == 0:
-                nc.vector.tensor_copy(grouped[:, m], part)
+                nc.vector.tensor_copy(grouped[:], part)
             else:
-                nc.scalar.copy(grouped[:, m], part)
-            if o == 0:
-                codes = stage.tile([P, P], U32, name="q_codes_0_%d" % m, offset=AT_Q_CODES + m * CODES, align_bytes=64)
+                nc.scalar.copy(grouped[:], part)
+            if o == 0 and m > 0:
+                codes = stage.tile([P, P], U32, name="q_codes_0_%d" % m, offset=AT_C_BYTES + m * 4 * P, align_bytes=64)
             else:
-                codes = keep.tile([P, P], U32, name="q_codes_1_%d" % m, align_bytes=64)
+                codes = keep.tile([P, P], U32, name="q_codes_%d_%d" % (o, m), align_bytes=64)
             plane = keep.tile([P, P], U8, name="q_plane_%d_%d" % (o, m), align_bytes=64)
-            nc.vector.quantize_mx(out=codes[:].bitcast(FP8X4), scales=plane[:], in_=grouped[:, m].rearrange("p c j -> p (c j)"))
+            nc.vector.quantize_mx(out=codes[:].bitcast(FP8X4), scales=plane[:], in_=grouped[:].rearrange("p c j -> p (c j)"))
             return codes, plane
-
-        def grouped_queries(o):
-            return stage.tile([P, Q_TILES, P, PACK], BF16, name="q_grouped_%d" % o, offset=AT_Q_GROUPED, align_bytes=64)
 
         def score_pass(q_mx, m, table, o):
             codes, plane = q_mx
@@ -167,69 +144,67 @@ def tile_attend_at_resid_topk_kernel(tc, qT, k_words, k_scales, c_words, c_scale
             return turned
 
         q_first = []
-        q_grouped = grouped_queries(0)
         for m in range(Q_TILES):
-            q_first.append(quantise_queries(0, m, q_grouped))
+            q_first.append(quantise_queries(0, m))
             score_pass(q_first[m], m, 0, 0)
-        key_codes.append(part_words("c", gather_words("c", word_pools[1], AT_C_LISTED)))
+        key_codes.append(gather_words("c", word_pools[1]))
         for m in range(Q_TILES):
             score_pass(q_first[m], m, 1, 0)
-        q_grouped = grouped_queries(1)
         y_turned = []
         for m in range(Q_TILES):
-            q_second = quantise_queries(1, m, q_grouped)
+            q_second = quantise_queries(1, m)
             for table in range(2):
                 score_pass(q_second, m, table, 1)
             y_turned.append(turn_weights(m))
 
-        def load_values(j, slot):
-            v_pool = stage.tile([P, T], F32, name="v_pool_%d" % j, offset=slot)
-            nc.sync.dma_start(v_pool[:], vT[j * P : (j + 1) * P, :])
-            return v_pool
-
-        v_pools = [load_values(j, AT_V + j * PITCH) for j in range(E_TILES)]
-
         y_mx = []
 
-        def weights_of(pair, grouped):
-            for i in range(2):
-                nc.vector.tensor_tensor(
-                    grouped[:, i],
-                    y_turned[2 * pair + i][:].rearrange("s t q -> s q t"),
-                    us_cols[:].unsqueeze(1).to_broadcast([P, P, PACK]),
-                    MULT,
-                )
-            codes = keep.tile([P, 2 * P], U32, name="y_codes_%d" % pair, align_bytes=64)
-            plane = keep.tile([P, 2 * P], U8, name="y_plane_%d" % pair, align_bytes=64)
-            nc.vector.quantize_mx(out=codes[:].bitcast(FP8X4), scales=plane[:], in_=grouped[:].rearrange("s i q t -> s (i q t)"))
-            for i in range(2):
-                y_mx.append((codes[:, i * P : (i + 1) * P], plane[:, i * P : (i + 1) * P]))
+        def weights_of(m):
+            at = SLOT + m * 2 * N
+            grouped = stage.tile([P, P, PACK], BF16, name="y_grouped_%d" % m, offset=at, align_bytes=64)
+            nc.vector.tensor_tensor(
+                grouped[:],
+                y_turned[m][:].rearrange("s t q -> s q t"),
+                us_cols[:].unsqueeze(1).to_broadcast([P, P, PACK]),
+                MULT,
+            )
+            codes = keep.tile([P, P], U32, name="y_codes_%d" % m, align_bytes=64)
+            plane = keep.tile([P, P], U8, name="y_plane_%d" % m, align_bytes=64)
+            nc.vector.quantize_mx(out=codes[:].bitcast(FP8X4), scales=plane[:], in_=grouped[:].rearrange("s q t -> s (q t)"))
+            y_mx.append((codes[:], plane[:]))
 
-        def gather_values(j, at):
-            listed_v = stage.tile([P, N], BF16, name="listed_v_%d" % j, offset=at)
-            nc.vector.tensor_copy(listed_v[:], v_pools[j][:].indirect(offsets[:]))
+        def gather_values(j, on_vector):
+            listed_v = keep.tile([P, N], BF16, name="listed_v_%d" % j)
+            cut = on_vector // 16
+            if on_vector > 0:
+                nc.vector.tensor_copy(listed_v[:, 0:on_vector], v_pools[j][:].indirect(offsets[:, 0:cut]))
+            if on_vector < N:
+                nc.scalar.activation(listed_v[:, on_vector:N], v_pools[j][:].indirect(offsets[:, cut:LIST_COLS]), COPY)
             return listed_v
 
-        def turn_values(listed_v, grouped):
+        def turn_values(j, listed_v):
             pairs = listed_v[:].bitcast(F32)
             turned = psum.tile([P, PACK, P], F32, name="turned", bufs=4)
             for u in range(2):
                 nc.tensor.transpose(turned[:, u, :], pairs[:, u : N // 2 : 2], identity[:])
+            if j < E_TILES - 1:
+                at = max(j + 1, 2) * SLOT + (j % 2) * 2 * N
+                grouped = stage.tile([P, N], BF16, name="v_grouped_%d" % j, offset=at, align_bytes=64)
+            else:
+                grouped = keep.tile([P, N], BF16, name="v_grouped_%d" % j, align_bytes=64)
             nc.scalar.copy(
                 grouped[:].bitcast(F32).rearrange("s (e u) -> s e u", u=2),
                 turned[:, 0:2, :].rearrange("s u e -> s e u"),
             )
+            return grouped
 
         def quantise_values(j, grouped):
-            if 0 < j < E_TILES - 1:
-                at = AT_V + (j + 1) * PITCH + SLOT - EDGE
-                wide = stage.tile([P, (EDGE + CODES) // 4], U32, name="v_codes_%d" % j, offset=at, align_bytes=64)
-                codes = wide[:, EDGE // 4 :]
+            if j < 2:
+                codes = stage.tile([P, P], U32, name="v_codes_%d" % j, offset=3 * SLOT + 2 * N + j * 4 * P, align_bytes=64)
             else:
-                whole = keep.tile([P, P], U32, name="v_codes_%d" % j, align_bytes=64)
-                codes = whole[:]
+                codes = keep.tile([P, P], U32, name="v_codes_%d" % j, align_bytes=64)
             plane = keep.tile([P, P], U8, name="v_plane_%d" % j, align_bytes=64)
-            nc.vector.quantize_mx(out=codes.bitcast(FP8X4), scales=plane[:], in_=grouped[:])
+            nc.vector.quantize_mx(out=codes[:].bitcast(FP8X4), scales=plane[:], in_=grouped[:])
             return codes, plane
 
         out_rows = out[0].rearrange("(m q) e -> q m e", q=P)
@@ -242,38 +217,38 @@ def tile_attend_at_resid_topk_kernel(tc, qT, k_words, k_scales, c_words, c_scale
                     out=sums[:, i, :],
                     lhsT=codes.bitcast(FP8X4),
                     lhsT_scale=plane,
-                    rhs=v_codes.bitcast(FP8X4),
+                    rhs=v_codes[:].bitcast(FP8X4),
                     rhs_scale=v_plane[:],
                     start=True,
                     stop=True,
                 )
 
-        def finish_values(j, grouped):
-            v_mx = quantise_values(j, grouped)
+        def finish_values(j, v_mx):
             sums = psum.tile([P, Q_TILES, P], F32, name="sums_%d" % j, tag="scores_%d" % j)
             products(v_mx, sums, 0, Q_TILES)
-            staged = keep.tile([P, Q_TILES, P], F32, name="staged_%d" % j)
-            nc.scalar.copy(staged[:], sums[:])
+            if j < 2:
+                staged = stage.tile([P, Q_TILES, P], F32, name="staged_%d" % j, offset=3 * SLOT + (j + 1) * 4 * N)
+            else:
+                staged = keep.tile([P, Q_TILES, P], F32, name="staged_%d" % j)
+            if j == 1:
+                nc.vector.tensor_copy(staged[:], sums[:])
+            else:
+                nc.scalar.copy(staged[:], sums[:])
             nc.sync.dma_start(out_rows[:, :, j * P : (j + 1) * P], staged[:])
 
-        listed_v = gather_values(0, AT_Q_GROUPED)
-        y_early = stage.tile([P, 2, P, PACK], BF16, name="y_early", offset=AT_V, align_bytes=64)
-        weights_of(0, y_early)
-        y_late = stage.tile([P, 2, P, PACK], BF16, name="y_late", offset=AT_Y_LATE, align_bytes=64)
-        weights_of(1, y_late)
-
-        v_grouped = [keep.tile([P, N], BF16, name="v_grouped_%d" % j, align_bytes=64) for j in (0, 2, 3)]
-        v_grouped = [v_grouped[0], stage.tile([P, N], BF16, name="v_grouped_1", offset=AT_V_SECOND, align_bytes=64)] + v_grouped[1:]
-        turn_values(listed_v, v_grouped[0])
-        finish_values(0, v_grouped[0])
-        turn_values(gather_values(1, AT_Y_LATE), v_grouped[1])
-        turn_values(gather_values(2, AT_Y_LATE + GROUPED), v_grouped[2])
-        finish_values(1, v_grouped[1])
-        turn_values(gather_values(3, AT_V_SECOND), v_grouped[3])
-        finish_values(2, v_grouped[2])
-
+        listed_v = [gather_values(0, N), gather_values(1, N)]
+        for m in range(Q_TILES):
+            weights_of(m)
+        listed_v.append(gather_values(2, 0))
+        v_grouped = [turn_values(i, listed_v[i]) for i in range(2)]
         j = E_TILES - 1
+        listed_v.append(gather_values(j, N // 2))
+        v_early = [quantise_values(i, v_grouped[i]) for i in range(2)]
+        v_grouped += [turn_values(i, listed_v[i]) for i in range(2, E_TILES)]
+        v_early.append(quantise_values(2, v_grouped[2]))
         v_mx = quantise_values(j, v_grouped[j])
+        for i in range(E_TILES - 1):
+            finish_values(i, v_early[i])
         low = psum.tile([P, 2, P], F32, name="low", tag="scores_%d" % j)
         products(v_mx, low, 0, 2)
         high = psum.tile([P, 2, P], F32, name="high", tag="scores_0")

@@ -26,6 +26,9 @@ SHIFT = 16
 SLOT = 4 * T
 AT_K_BYTES = E_TILES * SLOT
 AT_C_BYTES = AT_K_BYTES + T
+AT_K_WORDS = AT_C_BYTES + T
+AT_C_WORDS = AT_K_WORDS + SLOT
+AT_Q = AT_C_WORDS + SLOT
 
 FLOPS = 2 * N * NQ * (2 * D + DV)
 
@@ -34,15 +37,13 @@ def tile_attend_at_resid_topk_kernel(tc, qT, k_words, k_scales, c_words, c_scale
     nc = tc.nc
     with ExitStack() as ctx:
         keep = ctx.enter_context(tc.tile_pool(name="keep", bufs=1))
-        ring = ctx.enter_context(tc.tile_pool(name="ring", bufs=2))
         stage = ctx.enter_context(tc.tile_pool(name="stage", bufs=1))
         psum = ctx.enter_context(tc.psum_pool(name="psum", bufs=1))
 
         offsets = keep.tile([P, LIST_COLS], U16, name="offsets")
-        nc.sync.dma_start(offsets[:], offs)
 
-        def load_words(name, words):
-            pool_words = keep.tile([P, T], I32, name=name + "_pool_words")
+        def load_words(name, words, at):
+            pool_words = stage.tile([P, T], I32, name=name + "_pool_words", offset=at)
             nc.sync.dma_start(pool_words[:], words[0].rearrange("p t b -> p (t b)").bitcast(I32))
             return pool_words
 
@@ -55,16 +56,17 @@ def tile_attend_at_resid_topk_kernel(tc, qT, k_words, k_scales, c_words, c_scale
             return pool_bytes
 
         def load_queries(o):
-            raw = keep.tile([P, PACK, NQ], F32, name="q_raw_%d" % o)
+            raw = stage.tile([P, PACK, NQ], F32, name="q_raw_%d" % o, offset=AT_Q + o * SLOT)
             rows = qT[0, o * P * PACK : (o + 1) * P * PACK, :]
             nc.sync.dma_start(raw[:], rows.rearrange("(p j) c -> p j c", j=PACK))
             return raw
 
-        word_pools = [load_words("k", k_words)]
+        word_pools = [load_words("k", k_words, AT_K_WORDS)]
+        nc.sync.dma_start(offsets[:], offs)
         byte_pools = [load_bytes("k", k_scales, nc.gpsimd, AT_K_BYTES)]
         q_raw = [load_queries(0)]
         byte_pools.append(load_bytes("c", c_scales, nc.vector, AT_C_BYTES))
-        word_pools.append(load_words("c", c_words))
+        word_pools.append(load_words("c", c_words, AT_C_WORDS))
         q_raw.append(load_queries(1))
 
         padded = keep.tile([P, P], F32, name="padded")
@@ -77,16 +79,17 @@ def tile_attend_at_resid_topk_kernel(tc, qT, k_words, k_scales, c_words, c_scale
         nc.gpsimd.dma_start(us_cols[:], us[0].rearrange("(p t) one -> p (t one)", t=PACK))
         ls_turned = psum.tile([P, PACK, P], F32, name="turned", bufs=4)
         nc.tensor.transpose(ls_turned[:, 0, :], padded[:], identity[:])
-        neg_ls = keep.tile([P, Q_TILES], F32, name="neg_ls")
-        nc.scalar.activation(neg_ls[:], ls_turned[:, 0, 0:Q_TILES], COPY, scale=-1.0)
 
 
         def gather_words(name, pool_words):
             listed_words = keep.tile([P, N], U32, name=name + "_listed_words")
             nc.vector.tensor_copy(listed_words[:], pool_words[:].bitcast(U32).indirect(offsets[:]))
-            halves = keep.tile([P, PASSES, N], U16, name=name + "_halves", align_bytes=64)
-            nc.vector.tensor_copy(halves[:], listed_words[:].bitcast(U16).rearrange("p (n o) -> p o n", o=PASSES))
-            return halves
+            return listed_words
+
+        def part_words(name, listed_words, o):
+            half = keep.tile([P, N], U16, name=name + "_half_%d" % o, align_bytes=64)
+            nc.vector.tensor_copy(half[:], listed_words[:].bitcast(U16)[:, o : PASSES * N : PASSES])
+            return half
 
         def gather_bytes(name, pool_bytes):
             listed_bytes = keep.tile([P, N], U8, name=name + "_listed_bytes", align_bytes=64)
@@ -96,7 +99,8 @@ def tile_attend_at_resid_topk_kernel(tc, qT, k_words, k_scales, c_words, c_scale
             nc.sync.dma_start(moved_bytes[0 : P - SHIFT, :].bitcast(I32), listed_bytes[SHIFT:P, :].bitcast(I32))
             return (listed_bytes, moved_bytes)
 
-        key_codes = [gather_words("k", word_pools[0])]
+        listed_k = gather_words("k", word_pools[0])
+        key_codes = [[part_words("k", listed_k, o) for o in range(PASSES)]]
         key_planes = [gather_bytes("k", byte_pools[0])]
         key_planes.append(gather_bytes("c", byte_pools[1]))
 
@@ -115,8 +119,9 @@ def tile_attend_at_resid_topk_kernel(tc, qT, k_words, k_scales, c_words, c_scale
                 nc.vector.tensor_copy(grouped[:], part)
             else:
                 nc.scalar.copy(grouped[:], part)
-            if o == 0 and m > 0:
-                codes = stage.tile([P, P], U32, name="q_codes_0_%d" % m, offset=AT_C_BYTES + m * 4 * P, align_bytes=64)
+            if o == 0:
+                at = AT_C_BYTES + m * 4 * P
+                codes = stage.tile([P, P], U32, name="q_codes_0_%d" % m, offset=at, align_bytes=64)
             else:
                 codes = keep.tile([P, P], U32, name="q_codes_%d_%d" % (o, m), align_bytes=64)
             plane = keep.tile([P, P], U8, name="q_plane_%d_%d" % (o, m), align_bytes=64)
@@ -129,38 +134,24 @@ def tile_attend_at_resid_topk_kernel(tc, qT, k_words, k_scales, c_words, c_scale
                 out=banks[m][:],
                 lhsT=codes[:].bitcast(FP8X4),
                 lhsT_scale=plane[:],
-                rhs=key_codes[table][:, o, :].bitcast(FP4X4),
+                rhs=key_codes[table][o][:].bitcast(FP4X4),
                 rhs_scale=key_planes[table][o][:],
                 start=(table == 0 and o == 0),
                 stop=(table == 1 and o == PASSES - 1),
             )
 
         def turn_weights(m):
-            dealt = ring.tile([P, PACK, P], F32, name="dealt")
+            dealt = keep.tile([P, PACK, P], F32, name="dealt_%d" % m)
             nc.scalar.activation(dealt[:], banks[m][:].rearrange("q (s t) -> q t s", t=PACK), EXP, bias=neg_ls[:, m : m + 1])
             turned = psum.tile([P, PACK, P], F32, name="turned", bufs=4)
             for t in range(PACK):
                 nc.tensor.transpose(turned[:, t, :], dealt[:, t, :], identity[:])
             return turned
 
-        q_first = []
-        for m in range(Q_TILES):
-            q_first.append(quantise_queries(0, m))
-            score_pass(q_first[m], m, 0, 0)
-        key_codes.append(gather_words("c", word_pools[1]))
-        for m in range(Q_TILES):
-            score_pass(q_first[m], m, 1, 0)
-        y_turned = []
-        for m in range(Q_TILES):
-            q_second = quantise_queries(1, m)
-            for table in range(2):
-                score_pass(q_second, m, table, 1)
-            y_turned.append(turn_weights(m))
-
         y_mx = []
 
         def weights_of(m):
-            at = SLOT + m * 2 * N
+            at = m * 2 * N
             grouped = stage.tile([P, P, PACK], BF16, name="y_grouped_%d" % m, offset=at, align_bytes=64)
             nc.vector.tensor_tensor(
                 grouped[:],
@@ -182,14 +173,31 @@ def tile_attend_at_resid_topk_kernel(tc, qT, k_words, k_scales, c_words, c_scale
                 nc.scalar.activation(listed_v[:, on_vector:N], v_pools[j][:].indirect(offsets[:, cut:LIST_COLS]), COPY)
             return listed_v
 
+        q_first = []
+        for m in range(Q_TILES):
+            q_first.append(quantise_queries(0, m))
+            score_pass(q_first[m], m, 0, 0)
+        listed_c = gather_words("c", word_pools[1])
+        key_codes.append([part_words("c", listed_c, o) for o in range(PASSES)])
+        neg_ls = stage.tile([P, Q_TILES], F32, name="neg_ls", offset=AT_Q)
+        nc.scalar.activation(neg_ls[:], ls_turned[:, 0, 0:Q_TILES], COPY, scale=-1.0)
+        for m in range(Q_TILES):
+            score_pass(q_first[m], m, 1, 0)
+        y_turned = []
+        for m in range(Q_TILES):
+            q_second = quantise_queries(1, m)
+            for table in range(2):
+                score_pass(q_second, m, table, 1)
+        for m in range(Q_TILES):
+            y_turned.append(turn_weights(m))
+
         def turn_values(j, listed_v):
             pairs = listed_v[:].bitcast(F32)
             turned = psum.tile([P, PACK, P], F32, name="turned", bufs=4)
             for u in range(2):
                 nc.tensor.transpose(turned[:, u, :], pairs[:, u : N // 2 : 2], identity[:])
-            if j < E_TILES - 1:
-                at = max(j + 1, 2) * SLOT + (j % 2) * 2 * N
-                grouped = stage.tile([P, N], BF16, name="v_grouped_%d" % j, offset=at, align_bytes=64)
+            if j < 2:
+                grouped = stage.tile([P, N], BF16, name="v_grouped_%d" % j, offset=2 * SLOT + j * 2 * N, align_bytes=64)
             else:
                 grouped = keep.tile([P, N], BF16, name="v_grouped_%d" % j, align_bytes=64)
             nc.scalar.copy(
@@ -199,8 +207,8 @@ def tile_attend_at_resid_topk_kernel(tc, qT, k_words, k_scales, c_words, c_scale
             return grouped
 
         def quantise_values(j, grouped):
-            if j < 2:
-                codes = stage.tile([P, P], U32, name="v_codes_%d" % j, offset=3 * SLOT + 2 * N + j * 4 * P, align_bytes=64)
+            if j == 2:
+                codes = stage.tile([P, P], U32, name="v_codes_%d" % j, offset=3 * SLOT, align_bytes=64)
             else:
                 codes = keep.tile([P, P], U32, name="v_codes_%d" % j, align_bytes=64)
             plane = keep.tile([P, P], U8, name="v_plane_%d" % j, align_bytes=64)
@@ -236,19 +244,21 @@ def tile_attend_at_resid_topk_kernel(tc, qT, k_words, k_scales, c_words, c_scale
                 nc.scalar.copy(staged[:], sums[:])
             nc.sync.dma_start(out_rows[:, :, j * P : (j + 1) * P], staged[:])
 
-        listed_v = [gather_values(0, N), gather_values(1, N)]
+        listed_first = gather_values(0, N)
         for m in range(Q_TILES):
             weights_of(m)
-        listed_v.append(gather_values(2, 0))
-        v_grouped = [turn_values(i, listed_v[i]) for i in range(2)]
+        listed_second = gather_values(1, 0)
+        listed_third = gather_values(2, 0)
+        v_first = quantise_values(0, turn_values(0, listed_first))
+        v_second = quantise_values(1, turn_values(1, listed_second))
+        grouped_third = turn_values(2, listed_third)
         j = E_TILES - 1
-        listed_v.append(gather_values(j, N // 2))
-        v_early = [quantise_values(i, v_grouped[i]) for i in range(2)]
-        v_grouped += [turn_values(i, listed_v[i]) for i in range(2, E_TILES)]
-        v_early.append(quantise_values(2, v_grouped[2]))
-        v_mx = quantise_values(j, v_grouped[j])
-        for i in range(E_TILES - 1):
-            finish_values(i, v_early[i])
+        listed_last = gather_values(j, N // 2)
+        finish_values(0, v_first)
+        finish_values(1, v_second)
+        v_third = quantise_values(2, grouped_third)
+        v_mx = quantise_values(j, turn_values(j, listed_last))
+        finish_values(2, v_third)
         low = psum.tile([P, 2, P], F32, name="low", tag="scores_%d" % j)
         products(v_mx, low, 0, 2)
         high = psum.tile([P, 2, P], F32, name="high", tag="scores_0")

@@ -87,7 +87,10 @@ def tile_attend_at_resid_topk_kernel(tc, qT, k_words, k_scales, c_words, c_scale
             return listed_words
 
         def part_words(name, listed_words, o):
-            half = keep.tile([P, N], U16, name=name + "_half_%d" % o, align_bytes=64)
+            if name == "k" and o == 1:
+                half = stage.tile([P, N], U16, name="k_half_1", offset=AT_C_WORDS, align_bytes=64)
+            else:
+                half = keep.tile([P, N], U16, name=name + "_half_%d" % o, align_bytes=64)
             nc.vector.tensor_copy(half[:], listed_words[:].bitcast(U16)[:, o : PASSES * N : PASSES])
             return half
 
@@ -100,7 +103,7 @@ def tile_attend_at_resid_topk_kernel(tc, qT, k_words, k_scales, c_words, c_scale
             return (listed_bytes, moved_bytes)
 
         listed_k = gather_words("k", word_pools[0])
-        key_codes = [[part_words("k", listed_k, o) for o in range(PASSES)]]
+        key_codes = [[part_words("k", listed_k, 0)]]
         key_planes = [gather_bytes("k", byte_pools[0])]
         key_planes.append(gather_bytes("c", byte_pools[1]))
 
@@ -113,9 +116,11 @@ def tile_attend_at_resid_topk_kernel(tc, qT, k_words, k_scales, c_words, c_scale
         banks = [psum.tile([P, N], F32, name="scores_%d" % m, tag="scores_%d" % m) for m in range(Q_TILES)]
 
         def quantise_queries(o, m):
-            grouped = keep.tile([P, P, PACK], BF16, name="q_grouped_%d_%d" % (o, m), align_bytes=64)
+            on_vector = (o == 1 and m % 2 == 0) or (o == 0 and m == Q_TILES - 1)
+            name = "q_grouped_vector" if on_vector else "q_grouped_%d_%d" % (o, m)
+            grouped = keep.tile([P, P, PACK], BF16, name=name, align_bytes=64)
             part = q_raw[o][:, :, m * P : (m + 1) * P].rearrange("p j c -> p c j")
-            if o == 1 and m % 2 == 0:
+            if on_vector:
                 nc.vector.tensor_copy(grouped[:], part)
             else:
                 nc.scalar.copy(grouped[:], part)
@@ -178,7 +183,9 @@ def tile_attend_at_resid_topk_kernel(tc, qT, k_words, k_scales, c_words, c_scale
             q_first.append(quantise_queries(0, m))
             score_pass(q_first[m], m, 0, 0)
         listed_c = gather_words("c", word_pools[1])
-        key_codes.append([part_words("c", listed_c, o) for o in range(PASSES)])
+        key_codes.append([part_words("c", listed_c, 0)])
+        key_codes[0].append(part_words("k", listed_k, 1))
+        key_codes[1].append(part_words("c", listed_c, 1))
         neg_ls = stage.tile([P, Q_TILES], F32, name="neg_ls", offset=AT_Q)
         nc.scalar.activation(neg_ls[:], ls_turned[:, 0, 0:Q_TILES], COPY, scale=-1.0)
         for m in range(Q_TILES):
@@ -196,19 +203,22 @@ def tile_attend_at_resid_topk_kernel(tc, qT, k_words, k_scales, c_words, c_scale
             turned = psum.tile([P, PACK, P], F32, name="turned", bufs=4)
             for u in range(2):
                 nc.tensor.transpose(turned[:, u, :], pairs[:, u : N // 2 : 2], identity[:])
-            if j < 2:
-                grouped = stage.tile([P, N], BF16, name="v_grouped_%d" % j, offset=2 * SLOT + j * 2 * N, align_bytes=64)
+            if j < E_TILES - 1:
+                at = (3 * SLOT if j == 2 else SLOT) + j * 2 * N
+                grouped = stage.tile([P, N], BF16, name="v_grouped_%d" % j, offset=at, align_bytes=64)
             else:
                 grouped = keep.tile([P, N], BF16, name="v_grouped_%d" % j, align_bytes=64)
-            nc.scalar.copy(
-                grouped[:].bitcast(F32).rearrange("s (e u) -> s e u", u=2),
-                turned[:, 0:2, :].rearrange("s u e -> s e u"),
-            )
+            words = grouped[:].bitcast(F32).rearrange("s (e u) -> s e u", u=2)
+            if j < 2:
+                nc.vector.tensor_copy(words, turned[:, 0:2, :].rearrange("s u e -> s e u"))
+            else:
+                nc.scalar.copy(words, turned[:, 0:2, :].rearrange("s u e -> s e u"))
             return grouped
 
         def quantise_values(j, grouped):
-            if j == 2:
-                codes = stage.tile([P, P], U32, name="v_codes_%d" % j, offset=3 * SLOT, align_bytes=64)
+            if j < 2:
+                at = 2 * SLOT + j * 4 * P
+                codes = stage.tile([P, P], U32, name="v_codes_%d" % j, offset=at, align_bytes=64)
             else:
                 codes = keep.tile([P, P], U32, name="v_codes_%d" % j, align_bytes=64)
             plane = keep.tile([P, P], U8, name="v_plane_%d" % j, align_bytes=64)
@@ -235,7 +245,7 @@ def tile_attend_at_resid_topk_kernel(tc, qT, k_words, k_scales, c_words, c_scale
             sums = psum.tile([P, Q_TILES, P], F32, name="sums_%d" % j, tag="scores_%d" % j)
             products(v_mx, sums, 0, Q_TILES)
             if j < 2:
-                staged = stage.tile([P, Q_TILES, P], F32, name="staged_%d" % j, offset=3 * SLOT + (j + 1) * 4 * N)
+                staged = stage.tile([P, Q_TILES, P], F32, name="staged_%d" % j, offset=3 * SLOT + (j + 2) * 4 * N)
             else:
                 staged = keep.tile([P, Q_TILES, P], F32, name="staged_%d" % j)
             if j == 1:
@@ -249,11 +259,13 @@ def tile_attend_at_resid_topk_kernel(tc, qT, k_words, k_scales, c_words, c_scale
             weights_of(m)
         listed_second = gather_values(1, 0)
         listed_third = gather_values(2, 0)
-        v_first = quantise_values(0, turn_values(0, listed_first))
-        v_second = quantise_values(1, turn_values(1, listed_second))
-        grouped_third = turn_values(2, listed_third)
+        grouped_first = turn_values(0, listed_first)
+        grouped_second = turn_values(1, listed_second)
+        v_first = quantise_values(0, grouped_first)
+        v_second = quantise_values(1, grouped_second)
         j = E_TILES - 1
-        listed_last = gather_values(j, N // 2)
+        listed_last = gather_values(j, 3 * N // 8)
+        grouped_third = turn_values(2, listed_third)
         finish_values(0, v_first)
         finish_values(1, v_second)
         v_third = quantise_values(2, grouped_third)

@@ -22,7 +22,6 @@ PASSES = D // (P * PACK)
 Q_TILES = NQ // P
 E_TILES = DV // P
 LIST_COLS = N // 16
-SHIFT = 16
 SLOT = 4 * T
 AT_K_BYTES = E_TILES * SLOT
 AT_C_BYTES = AT_K_BYTES + T
@@ -49,10 +48,9 @@ def tile_attend_at_resid_topk_kernel(tc, qT, k_words, k_scales, c_words, c_scale
 
         def load_bytes(name, scales, engine, at):
             pool_bytes = stage.tile([P, T], U8, name=name + "_pool_bytes", offset=at)
-            engine.memset(pool_bytes[:].bitcast(I32), 0)
-            rows = scales.rearrange("o (a r) t -> r a o t", r=4)
-            for r in range(4):
-                nc.sync.dma_start(pool_bytes[r:P:SHIFT, :].bitcast(I32), rows[r].bitcast(I32))
+            nc.sync.dma_start(pool_bytes[0:32, :].bitcast(I32), scales.rearrange("o f t -> f o t").bitcast(I32))
+            engine.memset(pool_bytes[32:64, :].bitcast(I32), 0)
+            engine.memset(pool_bytes[64:P, :].bitcast(I32), 0)
             return pool_bytes
 
         def load_queries(o):
@@ -61,22 +59,34 @@ def tile_attend_at_resid_topk_kernel(tc, qT, k_words, k_scales, c_words, c_scale
             nc.sync.dma_start(raw[:], rows.rearrange("(p j) c -> p j c", j=PACK))
             return raw
 
-        word_pools = [load_words("k", k_words, AT_K_WORDS)]
         nc.sync.dma_start(offsets[:], offs)
-        byte_pools = [load_bytes("k", k_scales, nc.gpsimd, AT_K_BYTES)]
+        us_cols = keep.tile([P, PACK], F32, name="us_cols")
+        nc.gpsimd.dma_start(us_cols[:], us[0].rearrange("(p t) one -> p (t one)", t=PACK))
+        byte_pools = [load_bytes("k", k_scales, nc.vector, AT_K_BYTES)]
+        byte_pools.append(load_bytes("c", c_scales, nc.gpsimd, AT_C_BYTES))
+        padded = keep.tile([P, P], F32, name="padded")
+        nc.vector.memset(padded[:], 0.0)
+        word_pools = [load_words("k", k_words, AT_K_WORDS)]
         q_raw = [load_queries(0)]
-        byte_pools.append(load_bytes("c", c_scales, nc.vector, AT_C_BYTES))
+
+        def lay_planes(name, pool_bytes):
+            listed_bytes = keep.tile([P, N], U8, name=name + "_listed_bytes", align_bytes=64)
+            laid = keep.tile([P, PASSES, N], U8, name=name + "_planes", align_bytes=64)
+            nc.vector.memset(laid[:].rearrange("p o n -> p (o n)").bitcast(I32), 0)
+            nc.vector.tensor_copy(listed_bytes[:], pool_bytes[:].indirect(offsets[:]))
+            for quad in range(4):
+                nc.sync.dma_start(laid[32 * quad : 32 * quad + 4].bitcast(I32), listed_bytes[8 * quad : 8 * quad + 8].bitcast(I32))
+            return laid
+
+        planes = [lay_planes("k", byte_pools[0])]
         word_pools.append(load_words("c", c_words, AT_C_WORDS))
+        planes.append(lay_planes("c", byte_pools[1]))
+        nc.sync.dma_start(padded[0:Q_TILES, :], ls[0, 0].rearrange("(m p) -> m p", p=P))
         q_raw.append(load_queries(1))
 
-        padded = keep.tile([P, P], F32, name="padded")
-        nc.gpsimd.memset(padded[:], 0.0)
-        nc.gpsimd.dma_start(padded[0:Q_TILES, :], ls[0, 0].rearrange("(m p) -> m p", p=P))
         identity = keep.tile([P, P], F32, name="identity")
         make_identity(nc, identity[:])
 
-        us_cols = keep.tile([P, PACK], F32, name="us_cols")
-        nc.gpsimd.dma_start(us_cols[:], us[0].rearrange("(p t) one -> p (t one)", t=PACK))
         ls_turned = psum.tile([P, PACK, P], F32, name="turned", bufs=4)
         nc.tensor.transpose(ls_turned[:, 0, :], padded[:], identity[:])
 
@@ -94,18 +104,8 @@ def tile_attend_at_resid_topk_kernel(tc, qT, k_words, k_scales, c_words, c_scale
             nc.vector.tensor_copy(half[:], listed_words[:].bitcast(U16)[:, o : PASSES * N : PASSES])
             return half
 
-        def gather_bytes(name, pool_bytes):
-            listed_bytes = keep.tile([P, N], U8, name=name + "_listed_bytes", align_bytes=64)
-            nc.vector.tensor_copy(listed_bytes[:], pool_bytes[:].indirect(offsets[:]))
-            moved_bytes = keep.tile([P, N], U8, name=name + "_moved_bytes", align_bytes=64)
-            nc.vector.memset(moved_bytes[:].bitcast(I32), 0)
-            nc.sync.dma_start(moved_bytes[0 : P - SHIFT, :].bitcast(I32), listed_bytes[SHIFT:P, :].bitcast(I32))
-            return (listed_bytes, moved_bytes)
-
         listed_k = gather_words("k", word_pools[0])
         key_codes = [[part_words("k", listed_k, 0)]]
-        key_planes = [gather_bytes("k", byte_pools[0])]
-        key_planes.append(gather_bytes("c", byte_pools[1]))
 
         def load_values(j):
             v_pool = stage.tile([P, T], F32, name="v_pool_%d" % j, offset=j * SLOT)
@@ -140,7 +140,7 @@ def tile_attend_at_resid_topk_kernel(tc, qT, k_words, k_scales, c_words, c_scale
                 lhsT=codes[:].bitcast(FP8X4),
                 lhsT_scale=plane[:],
                 rhs=key_codes[table][o][:].bitcast(FP4X4),
-                rhs_scale=key_planes[table][o][:],
+                rhs_scale=planes[table][:, o, :],
                 start=(table == 0 and o == 0),
                 stop=(table == 1 and o == PASSES - 1),
             )

@@ -46,11 +46,11 @@ def tile_attend_at_resid_topk_kernel(tc, qT, k_words, k_scales, c_words, c_scale
             nc.sync.dma_start(pool_words[:], words[0].rearrange("p t b -> p (t b)").bitcast(I32))
             return pool_words
 
-        def load_bytes(name, scales, engine, at):
+        def load_bytes(name, scales, engine, at, first):
             pool_bytes = stage.tile([P, T], U8, name=name + "_pool_bytes", offset=at)
-            nc.sync.dma_start(pool_bytes[0:32, :].bitcast(I32), scales.rearrange("o f t -> f o t").bitcast(I32))
-            engine.memset(pool_bytes[32:64, :].bitcast(I32), 0)
-            engine.memset(pool_bytes[64:P, :].bitcast(I32), 0)
+            nc.sync.dma_start(pool_bytes[first : first + 32, :].bitcast(I32), scales.rearrange("o f t -> f o t").bitcast(I32))
+            engine.memset(pool_bytes[first + 32 : first + 64, :].bitcast(I32), 0)
+            engine.memset(pool_bytes[64 - first : P - first, :].bitcast(I32), 0)
             return pool_bytes
 
         def load_queries(o):
@@ -62,25 +62,26 @@ def tile_attend_at_resid_topk_kernel(tc, qT, k_words, k_scales, c_words, c_scale
         nc.sync.dma_start(offsets[:], offs)
         us_cols = keep.tile([P, PACK], F32, name="us_cols")
         nc.gpsimd.dma_start(us_cols[:], us[0].rearrange("(p t) one -> p (t one)", t=PACK))
-        byte_pools = [load_bytes("k", k_scales, nc.vector, AT_K_BYTES)]
-        byte_pools.append(load_bytes("c", c_scales, nc.gpsimd, AT_C_BYTES))
+        byte_pools = [load_bytes("k", k_scales, nc.vector, AT_K_BYTES, 0)]
+        byte_pools.append(load_bytes("c", c_scales, nc.gpsimd, AT_C_BYTES, 64))
         padded = keep.tile([P, P], F32, name="padded")
         nc.vector.memset(padded[:], 0.0)
         word_pools = [load_words("k", k_words, AT_K_WORDS)]
         q_raw = [load_queries(0)]
 
-        def lay_planes(name, pool_bytes):
+        def lay_planes(name, pool_bytes, first):
             listed_bytes = keep.tile([P, N], U8, name=name + "_listed_bytes", align_bytes=64)
             laid = keep.tile([P, PASSES, N], U8, name=name + "_planes", align_bytes=64)
             nc.vector.memset(laid[:].rearrange("p o n -> p (o n)").bitcast(I32), 0)
             nc.vector.tensor_copy(listed_bytes[:], pool_bytes[:].indirect(offsets[:]))
-            for quad in range(4):
-                nc.sync.dma_start(laid[32 * quad : 32 * quad + 4].bitcast(I32), listed_bytes[8 * quad : 8 * quad + 8].bitcast(I32))
+            for quad in (0, 2, 1, 3):
+                rows = listed_bytes[first + 8 * quad : first + 8 * quad + 8]
+                nc.sync.dma_start(laid[32 * quad : 32 * quad + 4].bitcast(I32), rows.bitcast(I32))
             return laid
 
-        planes = [lay_planes("k", byte_pools[0])]
+        planes = [lay_planes("k", byte_pools[0], 0)]
         word_pools.append(load_words("c", c_words, AT_C_WORDS))
-        planes.append(lay_planes("c", byte_pools[1]))
+        planes.append(lay_planes("c", byte_pools[1], 64))
         nc.sync.dma_start(padded[0:Q_TILES, :], ls[0, 0].rearrange("(m p) -> m p", p=P))
         q_raw.append(load_queries(1))
 
@@ -97,15 +98,12 @@ def tile_attend_at_resid_topk_kernel(tc, qT, k_words, k_scales, c_words, c_scale
             return listed_words
 
         def part_words(name, listed_words, o):
-            if name == "k" and o == 1:
-                half = stage.tile([P, N], U16, name="k_half_1", offset=AT_C_WORDS, align_bytes=64)
-            else:
-                half = keep.tile([P, N], U16, name=name + "_half_%d" % o, align_bytes=64)
+            half = keep.tile([P, N], U16, name=name + "_half_%d" % o, align_bytes=64)
             nc.vector.tensor_copy(half[:], listed_words[:].bitcast(U16)[:, o : PASSES * N : PASSES])
             return half
 
         listed_k = gather_words("k", word_pools[0])
-        key_codes = [[part_words("k", listed_k, 0)]]
+        key_codes = [[part_words("k", listed_k, o) for o in range(PASSES)]]
 
         def load_values(j):
             v_pool = stage.tile([P, T], F32, name="v_pool_%d" % j, offset=j * SLOT)
@@ -115,23 +113,26 @@ def tile_attend_at_resid_topk_kernel(tc, qT, k_words, k_scales, c_words, c_scale
         v_pools = [load_values(j) for j in range(E_TILES)]
         banks = [psum.tile([P, N], F32, name="scores_%d" % m, tag="scores_%d" % m) for m in range(Q_TILES)]
 
-        def quantise_queries(o, m):
-            on_vector = (o == 1 and m % 2 == 0) or (o == 0 and m == Q_TILES - 1)
-            name = "q_grouped_vector" if on_vector else "q_grouped_%d_%d" % (o, m)
-            grouped = keep.tile([P, P, PACK], BF16, name=name, align_bytes=64)
+        def group_queries(o, m):
+            grouped = keep.tile([P, P, PACK], BF16, name="q_grouped_%d_%d" % (o, m), align_bytes=64)
             part = q_raw[o][:, :, m * P : (m + 1) * P].rearrange("p j c -> p c j")
-            if on_vector:
+            if m % 2 == 0 or (o, m) == (1, 3):
                 nc.vector.tensor_copy(grouped[:], part)
             else:
                 nc.scalar.copy(grouped[:], part)
-            if o == 0:
-                at = AT_C_BYTES + m * 4 * P
-                codes = stage.tile([P, P], U32, name="q_codes_0_%d" % m, offset=at, align_bytes=64)
+            return grouped
+
+        def quantise(name, grouped, width, at=None):
+            if at is None:
+                codes = keep.tile([P, width], U32, name=name + "_codes", align_bytes=64)
             else:
-                codes = keep.tile([P, P], U32, name="q_codes_%d_%d" % (o, m), align_bytes=64)
-            plane = keep.tile([P, P], U8, name="q_plane_%d_%d" % (o, m), align_bytes=64)
-            nc.vector.quantize_mx(out=codes[:].bitcast(FP8X4), scales=plane[:], in_=grouped[:].rearrange("p c j -> p (c j)"))
+                codes = stage.tile([P, width], U32, name=name + "_codes", offset=at, align_bytes=64)
+            plane = keep.tile([P, width], U8, name=name + "_plane", align_bytes=64)
+            nc.vector.quantize_mx(out=codes[:].bitcast(FP8X4), scales=plane[:], in_=grouped)
             return codes, plane
+
+        def quantise_queries(o, m, grouped):
+            return quantise("q_%d_%d" % (o, m), grouped[:].rearrange("p c j -> p (c j)"), P)
 
         def score_pass(q_mx, m, table, o):
             codes, plane = q_mx
@@ -153,21 +154,16 @@ def tile_attend_at_resid_topk_kernel(tc, qT, k_words, k_scales, c_words, c_scale
                 nc.tensor.transpose(turned[:, t, :], dealt[:, t, :], identity[:])
             return turned
 
-        y_mx = []
-
-        def weights_of(m):
-            at = m * 2 * N
-            grouped = stage.tile([P, P, PACK], BF16, name="y_grouped_%d" % m, offset=at, align_bytes=64)
+        def scale_weights(m, pair):
             nc.vector.tensor_tensor(
-                grouped[:],
+                pair[:, m % 2],
                 y_turned[m][:].rearrange("s t q -> s q t"),
                 us_cols[:].unsqueeze(1).to_broadcast([P, P, PACK]),
                 MULT,
             )
-            codes = keep.tile([P, P], U32, name="y_codes_%d" % m, align_bytes=64)
-            plane = keep.tile([P, P], U8, name="y_plane_%d" % m, align_bytes=64)
-            nc.vector.quantize_mx(out=codes[:].bitcast(FP8X4), scales=plane[:], in_=grouped[:].rearrange("s q t -> s (q t)"))
-            y_mx.append((codes[:], plane[:]))
+
+        def quantise_weights(h, pair):
+            return quantise("y_%d" % h, pair[:].rearrange("s m q t -> s (m q t)"), 2 * P)
 
         def gather_values(j, on_vector):
             listed_v = keep.tile([P, N], BF16, name="listed_v_%d" % j)
@@ -178,106 +174,100 @@ def tile_attend_at_resid_topk_kernel(tc, qT, k_words, k_scales, c_words, c_scale
                 nc.scalar.activation(listed_v[:, on_vector:N], v_pools[j][:].indirect(offsets[:, cut:LIST_COLS]), COPY)
             return listed_v
 
+        q_grouped = [group_queries(0, m) for m in range(Q_TILES)]
         q_first = []
         for m in range(Q_TILES):
-            q_first.append(quantise_queries(0, m))
+            q_first.append(quantise_queries(0, m, q_grouped[m]))
             score_pass(q_first[m], m, 0, 0)
         listed_c = gather_words("c", word_pools[1])
-        key_codes.append([part_words("c", listed_c, 0)])
-        key_codes[0].append(part_words("k", listed_k, 1))
-        key_codes[1].append(part_words("c", listed_c, 1))
-        neg_ls = stage.tile([P, Q_TILES], F32, name="neg_ls", offset=AT_Q)
+        key_codes.append([part_words("c", listed_c, o) for o in range(PASSES)])
+        neg_ls = keep.tile([P, Q_TILES], F32, name="neg_ls")
         nc.scalar.activation(neg_ls[:], ls_turned[:, 0, 0:Q_TILES], COPY, scale=-1.0)
         for m in range(Q_TILES):
             score_pass(q_first[m], m, 1, 0)
         y_turned = []
+        q_grouped = [group_queries(1, m) for m in range(2)]
         for m in range(Q_TILES):
-            q_second = quantise_queries(1, m)
+            q_second = quantise_queries(1, m, q_grouped[m])
+            if m < 2:
+                q_grouped.append(group_queries(1, m + 2))
             for table in range(2):
                 score_pass(q_second, m, table, 1)
         for m in range(Q_TILES):
             y_turned.append(turn_weights(m))
 
-        def turn_values(j, listed_v):
+        def turn_values(listed_v, grouped, on_vector):
             pairs = listed_v[:].bitcast(F32)
             turned = psum.tile([P, PACK, P], F32, name="turned", bufs=4)
             for u in range(2):
                 nc.tensor.transpose(turned[:, u, :], pairs[:, u : N // 2 : 2], identity[:])
-            if j < E_TILES - 1:
-                at = (3 * SLOT if j == 2 else SLOT) + j * 2 * N
-                grouped = stage.tile([P, N], BF16, name="v_grouped_%d" % j, offset=at, align_bytes=64)
-            else:
-                grouped = keep.tile([P, N], BF16, name="v_grouped_%d" % j, align_bytes=64)
-            words = grouped[:].bitcast(F32).rearrange("s (e u) -> s e u", u=2)
-            if j < 2:
+            words = grouped.bitcast(F32).rearrange("s (e u) -> s e u", u=2)
+            if on_vector:
                 nc.vector.tensor_copy(words, turned[:, 0:2, :].rearrange("s u e -> s e u"))
             else:
                 nc.scalar.copy(words, turned[:, 0:2, :].rearrange("s u e -> s e u"))
-            return grouped
-
-        def quantise_values(j, grouped):
-            if j < 2:
-                at = 2 * SLOT + j * 4 * P
-                codes = stage.tile([P, P], U32, name="v_codes_%d" % j, offset=at, align_bytes=64)
-            else:
-                codes = keep.tile([P, P], U32, name="v_codes_%d" % j, align_bytes=64)
-            plane = keep.tile([P, P], U8, name="v_plane_%d" % j, align_bytes=64)
-            nc.vector.quantize_mx(out=codes[:].bitcast(FP8X4), scales=plane[:], in_=grouped[:])
-            return codes, plane
 
         out_rows = out[0].rearrange("(m q) e -> q m e", q=P)
 
         def products(v_mx, sums, first, count):
             v_codes, v_plane = v_mx
             for i in range(count):
-                codes, plane = y_mx[first + i]
+                codes, plane = y_mx[(first + i) // 2]
+                cols = slice((first + i) % 2 * P, ((first + i) % 2 + 1) * P)
                 nc.tensor.matmul_mx(
                     out=sums[:, i, :],
-                    lhsT=codes.bitcast(FP8X4),
-                    lhsT_scale=plane,
+                    lhsT=codes[:, cols].bitcast(FP8X4),
+                    lhsT_scale=plane[:, cols],
                     rhs=v_codes[:].bitcast(FP8X4),
                     rhs_scale=v_plane[:],
                     start=True,
                     stop=True,
                 )
 
-        def finish_values(j, v_mx):
-            sums = psum.tile([P, Q_TILES, P], F32, name="sums_%d" % j, tag="scores_%d" % j)
-            products(v_mx, sums, 0, Q_TILES)
-            if j < 2:
-                staged = stage.tile([P, Q_TILES, P], F32, name="staged_%d" % j, offset=3 * SLOT + (j + 2) * 4 * N)
-            else:
-                staged = keep.tile([P, Q_TILES, P], F32, name="staged_%d" % j)
-            if j == 1:
-                nc.vector.tensor_copy(staged[:], sums[:])
-            else:
-                nc.scalar.copy(staged[:], sums[:])
-            nc.sync.dma_start(out_rows[:, :, j * P : (j + 1) * P], staged[:])
-
         listed_first = gather_values(0, N)
-        for m in range(Q_TILES):
-            weights_of(m)
+        y_pairs = [stage.tile([P, 2, P, PACK], BF16, name="y_pair_%d" % h, offset=h * 4 * N, align_bytes=64) for h in range(2)]
+        for m in range(Q_TILES - 1):
+            scale_weights(m, y_pairs[m // 2])
+        y_mx = [quantise_weights(0, y_pairs[0])]
+        scale_weights(Q_TILES - 1, y_pairs[1])
+        y_mx.append(quantise_weights(1, y_pairs[1]))
+
         listed_second = gather_values(1, 0)
+        early = stage.tile([P, 2, N], BF16, name="v_grouped_early", offset=SLOT, align_bytes=64)
+        turn_values(listed_first, early[:, 0, :], False)
+        turn_values(listed_second, early[:, 1, :], True)
         listed_third = gather_values(2, 0)
-        grouped_first = turn_values(0, listed_first)
-        grouped_second = turn_values(1, listed_second)
-        v_first = quantise_values(0, grouped_first)
-        v_second = quantise_values(1, grouped_second)
-        j = E_TILES - 1
-        listed_last = gather_values(j, 3 * N // 8)
-        grouped_third = turn_values(2, listed_third)
-        finish_values(0, v_first)
-        finish_values(1, v_second)
-        v_third = quantise_values(2, grouped_third)
-        v_mx = quantise_values(j, turn_values(j, listed_last))
-        finish_values(2, v_third)
-        low = psum.tile([P, 2, P], F32, name="low", tag="scores_%d" % j)
-        products(v_mx, low, 0, 2)
+        third = keep.tile([P, N], BF16, name="v_grouped_third", align_bytes=64)
+        turn_values(listed_third, third[:], False)
+        v_early = quantise("v_early", early[:].rearrange("s j c -> s (j c)"), 2 * P, 2 * SLOT)
+        sums_early = []
+        for h in range(2):
+            sums_early.append(psum.tile([P, 2, 2 * P], F32, name="sums_early_%d" % h, tag="scores_%d" % h))
+            products(v_early, sums_early[h], 2 * h, 2)
+
+        listed_last = gather_values(3, 5 * N // 8)
+        v_third = quantise("v_third", third[:], P, 3 * SLOT)
+        staged_a = stage.tile([P, 2, 2 * P], F32, name="staged_a", offset=3 * SLOT + 8 * N)
+        nc.vector.tensor_copy(staged_a[:], sums_early[0][:])
+        nc.sync.dma_start(out_rows[:, 0:2, 0 : 2 * P], staged_a[:])
+        staged_b = stage.tile([P, 2, 2 * P], F32, name="staged_b", offset=3 * SLOT + 4 * N)
+        nc.scalar.copy(staged_b[:], sums_early[1][:])
+        nc.sync.dma_start(out_rows[:, 2:4, 0 : 2 * P], staged_b[:])
+        last = keep.tile([P, N], BF16, name="v_grouped_last", align_bytes=64)
+        turn_values(listed_last, last[:], False)
+        v_last = quantise("v_last", last[:], P)
+        sums_third = psum.tile([P, Q_TILES, P], F32, name="sums_third", tag="scores_2")
+        products(v_third, sums_third, 0, Q_TILES)
+        staged_third = keep.tile([P, Q_TILES, P], F32, name="staged_third")
+        nc.scalar.copy(staged_third[:], sums_third[:])
+        nc.sync.dma_start(out_rows[:, :, 2 * P : 3 * P], staged_third[:])
+        low = psum.tile([P, 2, P], F32, name="low", tag="scores_3")
+        products(v_last, low, 0, 2)
         high = psum.tile([P, 2, P], F32, name="high", tag="scores_0")
-        products(v_mx, high, 2, 2)
+        products(v_last, high, 2, 2)
         staged_low = keep.tile([P, 2, P], F32, name="staged_low")
         nc.vector.tensor_copy(staged_low[:], low[:])
-        nc.sync.dma_start(out_rows[:, 0:2, j * P : (j + 1) * P], staged_low[:])
+        nc.sync.dma_start(out_rows[:, 0:2, 3 * P : 4 * P], staged_low[:])
         staged_high = keep.tile([P, 2, P], F32, name="staged_high")
         nc.scalar.copy(staged_high[:], high[:])
-        nc.scalar.dma_start(out_rows[:, 2:4, j * P : (j + 1) * P], staged_high[:])
+        nc.scalar.dma_start(out_rows[:, 2:4, 3 * P : 4 * P], staged_high[:])

@@ -60,35 +60,37 @@ def tile_attend_at_resid_topk_kernel(tc, qT, k_words, k_scales, c_words, c_scale
             return raw
 
         nc.sync.dma_start(offsets[:], offs)
+        byte_pools = [load_bytes("k", k_scales, nc.vector, AT_K_BYTES, 0)]
+        byte_pools.append(load_bytes("c", c_scales, nc.gpsimd, AT_C_BYTES, 0))
+        padded = keep.tile([P, P], F32, name="padded")
+        nc.gpsimd.memset(padded[:], 0.0)
+        nc.gpsimd.dma_start(padded[0:Q_TILES, :], ls[0, 0].rearrange("(m p) -> m p", p=P))
         us_cols = keep.tile([P, PACK], F32, name="us_cols")
         nc.gpsimd.dma_start(us_cols[:], us[0].rearrange("(p t) one -> p (t one)", t=PACK))
-        byte_pools = [load_bytes("k", k_scales, nc.vector, AT_K_BYTES, 0)]
-        byte_pools.append(load_bytes("c", c_scales, nc.gpsimd, AT_C_BYTES, 64))
-        padded = keep.tile([P, P], F32, name="padded")
-        nc.vector.memset(padded[:], 0.0)
         word_pools = [load_words("k", k_words, AT_K_WORDS)]
         q_raw = [load_queries(0)]
 
-        def lay_planes(name, pool_bytes, first):
-            listed_bytes = keep.tile([P, N], U8, name=name + "_listed_bytes", align_bytes=64)
-            laid = keep.tile([P, PASSES, N], U8, name=name + "_planes", align_bytes=64)
-            nc.vector.memset(laid[:].rearrange("p o n -> p (o n)").bitcast(I32), 0)
-            nc.vector.tensor_copy(listed_bytes[:], pool_bytes[:].indirect(offsets[:]))
-            for quad in (0, 2, 1, 3):
-                rows = listed_bytes[first + 8 * quad : first + 8 * quad + 8]
-                nc.sync.dma_start(laid[32 * quad : 32 * quad + 4].bitcast(I32), rows.bitcast(I32))
-            return laid
-
-        planes = [lay_planes("k", byte_pools[0], 0)]
-        word_pools.append(load_words("c", c_words, AT_C_WORDS))
-        planes.append(lay_planes("c", byte_pools[1], 64))
-        nc.sync.dma_start(padded[0:Q_TILES, :], ls[0, 0].rearrange("(m p) -> m p", p=P))
+        c_pool = stage.tile([P, T], I32, name="c_pool_words", offset=AT_C_WORDS)
+        c_rows = c_words[0].rearrange("p t b -> p (t b)").bitcast(I32)
+        nc.sync.dma_start(c_pool[:, 0 : T // 2], c_rows[:, 0 : T // 2])
+        word_pools.append(c_pool)
+        listed_bytes = keep.tile([P, 2, N], U8, name="listed_bytes", align_bytes=64)
+        planes = keep.tile([P, PASSES, 2, N], U8, name="planes", align_bytes=64)
+        nc.vector.memset(planes[:].rearrange("p o t n -> p (o t n)").bitcast(I32), 0)
+        for table in range(2):
+            nc.vector.tensor_copy(listed_bytes[:, table, :], byte_pools[table][:].indirect(offsets[:]))
+        for quad in (0, 2, 1, 3):
+            nc.sync.dma_start(
+                planes[32 * quad : 32 * quad + 4].rearrange("p o t n -> p o (t n)").bitcast(I32),
+                listed_bytes[8 * quad : 8 * quad + 8].rearrange("p t n -> p (t n)").bitcast(I32),
+            )
+        nc.sync.dma_start(c_pool[:, T // 2 : T], c_rows[:, T // 2 : T])
         q_raw.append(load_queries(1))
 
         identity = keep.tile([P, P], F32, name="identity")
         make_identity(nc, identity[:])
 
-        ls_turned = psum.tile([P, PACK, P], F32, name="turned", bufs=4)
+        ls_turned = psum.tile([P, PACK, P], F32, name="ls_turned", tag="turned_3")
         nc.tensor.transpose(ls_turned[:, 0, :], padded[:], identity[:])
 
 
@@ -131,17 +133,22 @@ def tile_attend_at_resid_topk_kernel(tc, qT, k_words, k_scales, c_words, c_scale
             nc.vector.quantize_mx(out=codes[:].bitcast(FP8X4), scales=plane[:], in_=grouped)
             return codes, plane
 
+        q_codes = [keep.tile([P, NQ], U32, name="q_codes_%d" % o, align_bytes=64) for o in range(PASSES)]
+        q_planes = [keep.tile([P, NQ], U8, name="q_plane_%d" % o, align_bytes=64) for o in range(PASSES)]
+
         def quantise_queries(o, m, grouped):
-            return quantise("q_%d_%d" % (o, m), grouped[:].rearrange("p c j -> p (c j)"), P)
+            codes, plane = q_codes[o][:, m * P : (m + 1) * P], q_planes[o][:, m * P : (m + 1) * P]
+            nc.vector.quantize_mx(out=codes.bitcast(FP8X4), scales=plane, in_=grouped[:].rearrange("p c j -> p (c j)"))
+            return codes, plane
 
         def score_pass(q_mx, m, table, o):
             codes, plane = q_mx
             nc.tensor.matmul_mx(
                 out=banks[m][:],
-                lhsT=codes[:].bitcast(FP8X4),
-                lhsT_scale=plane[:],
+                lhsT=codes.bitcast(FP8X4),
+                lhsT_scale=plane,
                 rhs=key_codes[table][o][:].bitcast(FP4X4),
-                rhs_scale=planes[table][:, o, :],
+                rhs_scale=planes[:, o, table, :],
                 start=(table == 0 and o == 0),
                 stop=(table == 1 and o == PASSES - 1),
             )
@@ -149,7 +156,7 @@ def tile_attend_at_resid_topk_kernel(tc, qT, k_words, k_scales, c_words, c_scale
         def turn_weights(m):
             dealt = keep.tile([P, PACK, P], F32, name="dealt_%d" % m)
             nc.scalar.activation(dealt[:], banks[m][:].rearrange("q (s t) -> q t s", t=PACK), EXP, bias=neg_ls[:, m : m + 1])
-            turned = psum.tile([P, PACK, P], F32, name="turned", bufs=4)
+            turned = psum.tile([P, PACK, P], F32, name="y_turned_%d" % m, tag="turned_%d" % m)
             for t in range(PACK):
                 nc.tensor.transpose(turned[:, t, :], dealt[:, t, :], identity[:])
             return turned
@@ -196,9 +203,9 @@ def tile_attend_at_resid_topk_kernel(tc, qT, k_words, k_scales, c_words, c_scale
         for m in range(Q_TILES):
             y_turned.append(turn_weights(m))
 
-        def turn_values(listed_v, grouped, on_vector):
+        def turn_values(j, listed_v, grouped, on_vector):
             pairs = listed_v[:].bitcast(F32)
-            turned = psum.tile([P, PACK, P], F32, name="turned", bufs=4)
+            turned = psum.tile([P, PACK, P], F32, name="v_turned_%d" % j, tag="turned_%d" % j)
             for u in range(2):
                 nc.tensor.transpose(turned[:, u, :], pairs[:, u : N // 2 : 2], identity[:])
             words = grouped.bitcast(F32).rearrange("s (e u) -> s e u", u=2)
@@ -226,19 +233,17 @@ def tile_attend_at_resid_topk_kernel(tc, qT, k_words, k_scales, c_words, c_scale
 
         listed_first = gather_values(0, N)
         y_pairs = [stage.tile([P, 2, P, PACK], BF16, name="y_pair_%d" % h, offset=h * 4 * N, align_bytes=64) for h in range(2)]
-        for m in range(Q_TILES - 1):
+        for m in range(Q_TILES):
             scale_weights(m, y_pairs[m // 2])
-        y_mx = [quantise_weights(0, y_pairs[0])]
-        scale_weights(Q_TILES - 1, y_pairs[1])
-        y_mx.append(quantise_weights(1, y_pairs[1]))
+        y_mx = [quantise_weights(h, y_pairs[h]) for h in range(2)]
 
         listed_second = gather_values(1, 0)
         early = stage.tile([P, 2, N], BF16, name="v_grouped_early", offset=SLOT, align_bytes=64)
-        turn_values(listed_first, early[:, 0, :], False)
-        turn_values(listed_second, early[:, 1, :], True)
+        turn_values(0, listed_first, early[:, 0, :], False)
+        turn_values(1, listed_second, early[:, 1, :], True)
         listed_third = gather_values(2, 0)
         third = keep.tile([P, N], BF16, name="v_grouped_third", align_bytes=64)
-        turn_values(listed_third, third[:], False)
+        turn_values(2, listed_third, third[:], False)
         v_early = quantise("v_early", early[:].rearrange("s j c -> s (j c)"), 2 * P, 2 * SLOT)
         sums_early = []
         for h in range(2):
@@ -254,7 +259,7 @@ def tile_attend_at_resid_topk_kernel(tc, qT, k_words, k_scales, c_words, c_scale
         nc.scalar.copy(staged_b[:], sums_early[1][:])
         nc.sync.dma_start(out_rows[:, 2:4, 0 : 2 * P], staged_b[:])
         last = keep.tile([P, N], BF16, name="v_grouped_last", align_bytes=64)
-        turn_values(listed_last, last[:], False)
+        turn_values(3, listed_last, last[:], False)
         v_last = quantise("v_last", last[:], P)
         sums_third = psum.tile([P, Q_TILES, P], F32, name="sums_third", tag="scores_2")
         products(v_third, sums_third, 0, Q_TILES)

@@ -241,6 +241,17 @@ def tile_attend_at_resid_topk_kernel(tc, qT, k_words, k_scales, c_words, c_scale
         early = stage.tile([P, 2, N], BF16, name="v_grouped_early", offset=SLOT, align_bytes=64)
         turn_values(0, listed_first, early[:, 0, :], False)
         turn_values(1, listed_second, early[:, 1, :], True)
+        warm = psum.tile([P, NQ], F32, name="warm", tag="turned_0")
+        for o in range(PASSES):
+            nc.tensor.matmul_mx(
+                out=warm[:],
+                lhsT=q_codes[o][:, 0:P].bitcast(FP8X4),
+                lhsT_scale=q_planes[o][:, 0:P],
+                rhs=q_codes[o][:].bitcast(FP8X4),
+                rhs_scale=q_planes[o][:],
+                start=(o == 0),
+                stop=(o == PASSES - 1),
+            )
         listed_third = gather_values(2, 0)
         third = keep.tile([P, N], BF16, name="v_grouped_third", align_bytes=64)
         turn_values(2, listed_third, third[:], False)

@@ -21,13 +21,18 @@ N, T, D, NQ, DV = 512, 2048, 1024, 512, 512
 PASSES = D // (P * PACK)
 Q_TILES = NQ // P
 E_TILES = DV // P
+HALF = NQ // 2
 LIST_COLS = N // 16
 SLOT = 4 * T
-AT_K_BYTES = E_TILES * SLOT
-AT_C_BYTES = AT_K_BYTES + T
-AT_K_WORDS = AT_C_BYTES + T
-AT_C_WORDS = AT_K_WORDS + SLOT
-AT_Q = AT_C_WORDS + SLOT
+SCALE_ROWS = 32
+FIRST_ROW = P - SCALE_ROWS
+SHARED = 5 * N // 8
+THIRD_SHARED = N // 2
+AT_Q = E_TILES * SLOT
+Q_BYTES = 4 * PACK * HALF
+AT_LAST_Q = AT_Q + 3 * Q_BYTES
+AT_LISTED = AT_Q + 4 * Q_BYTES
+AT_LAST_GROUPED = AT_LISTED + E_TILES * 2 * N
 
 FLOPS = 2 * N * NQ * (2 * D + DV)
 
@@ -40,40 +45,43 @@ def tile_attend_at_resid_topk_kernel(tc, qT, k_words, k_scales, c_words, c_scale
         psum = ctx.enter_context(tc.psum_pool(name="psum", bufs=1))
 
         offsets = keep.tile([P, LIST_COLS], U16, name="offsets")
+        nc.sync.dma_start(offsets[:], offs)
 
-        def load_words(name, words, at):
-            pool_words = stage.tile([P, T], I32, name=name + "_pool_words", offset=at)
+        def load_bytes(name, scales):
+            pool_bytes = keep.tile([P, T], U8, name=name + "_pool_bytes")
+            nc.sync.dma_start(pool_bytes[FIRST_ROW:P, :].bitcast(I32), scales.rearrange("o f t -> f o t").bitcast(I32))
+            nc.vector.memset(pool_bytes[0:FIRST_ROW, :].bitcast(I32), 0)
+            return pool_bytes
+
+        def load_words(name, words):
+            pool_words = keep.tile([P, T], I32, name=name + "_pool_words")
             nc.sync.dma_start(pool_words[:], words[0].rearrange("p t b -> p (t b)").bitcast(I32))
             return pool_words
 
-        def load_bytes(name, scales, engine, at, first):
-            pool_bytes = stage.tile([P, T], U8, name=name + "_pool_bytes", offset=at)
-            nc.sync.dma_start(pool_bytes[first : first + 32, :].bitcast(I32), scales.rearrange("o f t -> f o t").bitcast(I32))
-            engine.memset(pool_bytes[first + 32 : first + 64, :].bitcast(I32), 0)
-            engine.memset(pool_bytes[64 - first : P - first, :].bitcast(I32), 0)
-            return pool_bytes
-
-        def load_queries(o):
-            raw = stage.tile([P, PACK, NQ], F32, name="q_raw_%d" % o, offset=AT_Q + o * SLOT)
-            rows = qT[0, o * P * PACK : (o + 1) * P * PACK, :]
+        def load_queries(o, h):
+            raw = stage.tile([P, PACK, HALF], F32, name="q_raw_%d_%d" % (o, h), offset=AT_Q + (2 * h + o) * Q_BYTES)
+            rows = qT[0, o * P * PACK : (o + 1) * P * PACK, h * HALF : (h + 1) * HALF]
             nc.sync.dma_start(raw[:], rows.rearrange("(p j) c -> p j c", j=PACK))
             return raw
 
-        nc.sync.dma_start(offsets[:], offs)
-        byte_pools = [load_bytes("k", k_scales, nc.vector, AT_K_BYTES, 0)]
-        byte_pools.append(load_bytes("c", c_scales, nc.gpsimd, AT_C_BYTES, 0))
+        def load_values(j):
+            v_pool = stage.tile([P, T], F32, name="v_pool_%d" % j, offset=j * SLOT)
+            nc.sync.dma_start(v_pool[:], vT[j * P : (j + 1) * P, :])
+            return v_pool
+
+        byte_pools = [load_bytes("k", k_scales), load_bytes("c", c_scales)]
+        identity = keep.tile([P, P], F32, name="identity")
+        make_identity(nc, identity[:])
         padded = keep.tile([P, P], F32, name="padded")
         nc.gpsimd.memset(padded[:], 0.0)
         nc.gpsimd.dma_start(padded[0:Q_TILES, :], ls[0, 0].rearrange("(m p) -> m p", p=P))
         us_cols = keep.tile([P, PACK], F32, name="us_cols")
         nc.gpsimd.dma_start(us_cols[:], us[0].rearrange("(p t) one -> p (t one)", t=PACK))
-        word_pools = [load_words("k", k_words, AT_K_WORDS)]
-        q_raw = [load_queries(0)]
 
-        c_pool = stage.tile([P, T], I32, name="c_pool_words", offset=AT_C_WORDS)
-        c_rows = c_words[0].rearrange("p t b -> p (t b)").bitcast(I32)
-        nc.sync.dma_start(c_pool[:, 0 : T // 2], c_rows[:, 0 : T // 2])
-        word_pools.append(c_pool)
+        k_pool = load_words("k", k_words)
+        q_raw = {(0, 0): load_queries(0, 0)}
+        c_pool = load_words("c", c_words)
+
         listed_bytes = keep.tile([P, 2, N], U8, name="listed_bytes", align_bytes=64)
         planes = keep.tile([P, PASSES, 2, N], U8, name="planes", align_bytes=64)
         nc.vector.memset(planes[:].rearrange("p o t n -> p (o t n)").bitcast(I32), 0)
@@ -82,47 +90,78 @@ def tile_attend_at_resid_topk_kernel(tc, qT, k_words, k_scales, c_words, c_scale
         for quad in (0, 2, 1, 3):
             nc.sync.dma_start(
                 planes[32 * quad : 32 * quad + 4].rearrange("p o t n -> p o (t n)").bitcast(I32),
-                listed_bytes[8 * quad : 8 * quad + 8].rearrange("p t n -> p (t n)").bitcast(I32),
+                listed_bytes[FIRST_ROW + 8 * quad : FIRST_ROW + 8 * quad + 8].rearrange("p t n -> p (t n)").bitcast(I32),
             )
-        nc.sync.dma_start(c_pool[:, T // 2 : T], c_rows[:, T // 2 : T])
-        q_raw.append(load_queries(1))
+        for o, h in ((1, 0), (0, 1), (1, 1)):
+            q_raw[o, h] = load_queries(o, h)
+        v_pools = [load_values(j) for j in range(E_TILES)]
 
-        identity = keep.tile([P, P], F32, name="identity")
-        make_identity(nc, identity[:])
-
-        ls_turned = psum.tile([P, PACK, P], F32, name="ls_turned", tag="turned_3")
-        nc.tensor.transpose(ls_turned[:, 0, :], padded[:], identity[:])
-
+        ls_turned = psum.tile([P, P], F32, name="ls_turned", tag="x0")
+        nc.tensor.transpose(ls_turned[:], padded[:], identity[:])
+        neg_ls = keep.tile([P, Q_TILES], F32, name="neg_ls")
+        nc.scalar.activation(neg_ls[:], ls_turned[:, 0:Q_TILES], COPY, scale=-1.0)
 
         def gather_words(name, pool_words):
             listed_words = keep.tile([P, N], U32, name=name + "_listed_words")
             nc.vector.tensor_copy(listed_words[:], pool_words[:].bitcast(U32).indirect(offsets[:]))
-            return listed_words
+            halves = []
+            for o in range(PASSES):
+                half = keep.tile([P, N], U16, name=name + "_half_%d" % o, align_bytes=64)
+                nc.vector.tensor_copy(half[:], listed_words[:].bitcast(U16)[:, o : PASSES * N : PASSES])
+                halves.append(half)
+            return halves
 
-        def part_words(name, listed_words, o):
-            half = keep.tile([P, N], U16, name=name + "_half_%d" % o, align_bytes=64)
-            nc.vector.tensor_copy(half[:], listed_words[:].bitcast(U16)[:, o : PASSES * N : PASSES])
-            return half
+        q_codes = [keep.tile([P, NQ], U32, name="q_codes_%d" % o, align_bytes=64) for o in range(PASSES)]
+        q_planes = [keep.tile([P, NQ], U8, name="q_plane_%d" % o, align_bytes=64) for o in range(PASSES)]
 
-        listed_k = gather_words("k", word_pools[0])
-        key_codes = [[part_words("k", listed_k, o) for o in range(PASSES)]]
-
-        def load_values(j):
-            v_pool = stage.tile([P, T], F32, name="v_pool_%d" % j, offset=j * SLOT)
-            nc.sync.dma_start(v_pool[:], vT[j * P : (j + 1) * P, :])
-            return v_pool
-
-        v_pools = [load_values(j) for j in range(E_TILES)]
-        banks = [psum.tile([P, N], F32, name="scores_%d" % m, tag="scores_%d" % m) for m in range(Q_TILES)]
-
-        def group_queries(o, m):
-            grouped = keep.tile([P, P, PACK], BF16, name="q_grouped_%d_%d" % (o, m), align_bytes=64)
-            part = q_raw[o][:, :, m * P : (m + 1) * P].rearrange("p j c -> p c j")
-            if m % 2 == 0 or (o, m) == (1, 3):
+        def group_queries(o, first, count, on_vector):
+            grouped = keep.tile([P, count * P, PACK], BF16, name="q_grouped_%d_%d" % (o, first), align_bytes=64)
+            at = first % 2 * P
+            part = q_raw[o, first // 2][:, :, at : at + count * P].rearrange("p j c -> p c j")
+            if on_vector:
                 nc.vector.tensor_copy(grouped[:], part)
             else:
                 nc.scalar.copy(grouped[:], part)
             return grouped
+
+        def quantise_queries(o, first, count, grouped):
+            cols = slice(first * P, (first + count) * P)
+            nc.vector.quantize_mx(
+                out=q_codes[o][:, cols].bitcast(FP8X4), scales=q_planes[o][:, cols], in_=grouped[:].rearrange("p c j -> p (c j)")
+            )
+
+        banks = [psum.tile([P, N], F32, name="scores_%d" % m, tag="s%d" % m) for m in range(Q_TILES)]
+
+        def score_pass(m, table, o, start=False, stop=False):
+            cols = slice(m * P, (m + 1) * P)
+            nc.tensor.matmul_mx(
+                out=banks[m][:],
+                lhsT=q_codes[o][:, cols].bitcast(FP8X4),
+                lhsT_scale=q_planes[o][:, cols],
+                rhs=key_codes[table][o][:].bitcast(FP4X4),
+                rhs_scale=planes[:, o, table, :],
+                start=start,
+                stop=stop,
+            )
+
+        def exp_scores(m, at=None):
+            if at is None:
+                dealt = keep.tile([P, PACK, P], F32, name="dealt_%d" % m)
+            else:
+                dealt = stage.tile([P, PACK, P], F32, name="dealt_%d" % m, offset=at)
+            nc.scalar.activation(dealt[:], banks[m][:].rearrange("q (s t) -> q t s", t=PACK), EXP, bias=neg_ls[:, m : m + 1])
+            return dealt
+
+        def turn_weights(m, dealt, tag):
+            turned = psum.tile([P, PACK, P], F32, name="y_turned_%d" % m, tag=tag)
+            for t in range(PACK):
+                nc.tensor.transpose(turned[:, t, :], dealt[:, t, :], identity[:])
+            return turned
+
+        def scale_weights(turned, grouped):
+            nc.vector.tensor_tensor(
+                grouped, turned[:].rearrange("s t q -> s q t"), us_cols[:].unsqueeze(1).to_broadcast([P, P, PACK]), MULT
+            )
 
         def quantise(name, grouped, width, at=None):
             if at is None:
@@ -133,47 +172,8 @@ def tile_attend_at_resid_topk_kernel(tc, qT, k_words, k_scales, c_words, c_scale
             nc.vector.quantize_mx(out=codes[:].bitcast(FP8X4), scales=plane[:], in_=grouped)
             return codes, plane
 
-        q_codes = [keep.tile([P, NQ], U32, name="q_codes_%d" % o, align_bytes=64) for o in range(PASSES)]
-        q_planes = [keep.tile([P, NQ], U8, name="q_plane_%d" % o, align_bytes=64) for o in range(PASSES)]
-
-        def quantise_queries(o, m, grouped):
-            codes, plane = q_codes[o][:, m * P : (m + 1) * P], q_planes[o][:, m * P : (m + 1) * P]
-            nc.vector.quantize_mx(out=codes.bitcast(FP8X4), scales=plane, in_=grouped[:].rearrange("p c j -> p (c j)"))
-            return codes, plane
-
-        def score_pass(q_mx, m, table, o):
-            codes, plane = q_mx
-            nc.tensor.matmul_mx(
-                out=banks[m][:],
-                lhsT=codes.bitcast(FP8X4),
-                lhsT_scale=plane,
-                rhs=key_codes[table][o][:].bitcast(FP4X4),
-                rhs_scale=planes[:, o, table, :],
-                start=(table == 0 and o == 0),
-                stop=(table == 1 and o == PASSES - 1),
-            )
-
-        def turn_weights(m):
-            dealt = keep.tile([P, PACK, P], F32, name="dealt_%d" % m)
-            nc.scalar.activation(dealt[:], banks[m][:].rearrange("q (s t) -> q t s", t=PACK), EXP, bias=neg_ls[:, m : m + 1])
-            turned = psum.tile([P, PACK, P], F32, name="y_turned_%d" % m, tag="turned_%d" % m)
-            for t in range(PACK):
-                nc.tensor.transpose(turned[:, t, :], dealt[:, t, :], identity[:])
-            return turned
-
-        def scale_weights(m, pair):
-            nc.vector.tensor_tensor(
-                pair[:, m % 2],
-                y_turned[m][:].rearrange("s t q -> s q t"),
-                us_cols[:].unsqueeze(1).to_broadcast([P, P, PACK]),
-                MULT,
-            )
-
-        def quantise_weights(h, pair):
-            return quantise("y_%d" % h, pair[:].rearrange("s m q t -> s (m q t)"), 2 * P)
-
         def gather_values(j, on_vector):
-            listed_v = keep.tile([P, N], BF16, name="listed_v_%d" % j)
+            listed_v = stage.tile([P, N], BF16, name="listed_v_%d" % j, offset=AT_LISTED + j * 2 * N)
             cut = on_vector // 16
             if on_vector > 0:
                 nc.vector.tensor_copy(listed_v[:, 0:on_vector], v_pools[j][:].indirect(offsets[:, 0:cut]))
@@ -181,43 +181,23 @@ def tile_attend_at_resid_topk_kernel(tc, qT, k_words, k_scales, c_words, c_scale
                 nc.scalar.activation(listed_v[:, on_vector:N], v_pools[j][:].indirect(offsets[:, cut:LIST_COLS]), COPY)
             return listed_v
 
-        q_grouped = [group_queries(0, m) for m in range(Q_TILES)]
-        q_first = []
-        for m in range(Q_TILES):
-            q_first.append(quantise_queries(0, m, q_grouped[m]))
-            score_pass(q_first[m], m, 0, 0)
-        listed_c = gather_words("c", word_pools[1])
-        key_codes.append([part_words("c", listed_c, o) for o in range(PASSES)])
-        neg_ls = keep.tile([P, Q_TILES], F32, name="neg_ls")
-        nc.scalar.activation(neg_ls[:], ls_turned[:, 0, 0:Q_TILES], COPY, scale=-1.0)
-        for m in range(Q_TILES):
-            score_pass(q_first[m], m, 1, 0)
-        y_turned = []
-        q_grouped = [group_queries(1, m) for m in range(2)]
-        for m in range(Q_TILES):
-            q_second = quantise_queries(1, m, q_grouped[m])
-            if m < 2:
-                q_grouped.append(group_queries(1, m + 2))
-            for table in range(2):
-                score_pass(q_second, m, table, 1)
-        for m in range(Q_TILES):
-            y_turned.append(turn_weights(m))
-
-        def turn_values(j, listed_v, grouped, on_vector):
+        def turn_values(j, listed_v, tag):
             pairs = listed_v[:].bitcast(F32)
-            turned = psum.tile([P, PACK, P], F32, name="v_turned_%d" % j, tag="turned_%d" % j)
+            turned = psum.tile([P, 2, P], F32, name="v_turned_%d" % j, tag=tag)
             for u in range(2):
                 nc.tensor.transpose(turned[:, u, :], pairs[:, u : N // 2 : 2], identity[:])
+            return turned
+
+        def group_values(grouped, turned, on_vector):
             words = grouped.bitcast(F32).rearrange("s (e u) -> s e u", u=2)
             if on_vector:
-                nc.vector.tensor_copy(words, turned[:, 0:2, :].rearrange("s u e -> s e u"))
+                nc.vector.tensor_copy(words, turned[:].rearrange("s u e -> s e u"))
             else:
-                nc.scalar.copy(words, turned[:, 0:2, :].rearrange("s u e -> s e u"))
+                nc.scalar.copy(words, turned[:].rearrange("s u e -> s e u"))
 
-        out_rows = out[0].rearrange("(m q) e -> q m e", q=P)
-
-        def products(v_mx, sums, first, count):
+        def products(name, v_mx, first, count, tag, width=P):
             v_codes, v_plane = v_mx
+            sums = psum.tile([P, count, width], F32, name=name, tag=tag)
             for i in range(count):
                 codes, plane = y_mx[(first + i) // 2]
                 cols = slice((first + i) % 2 * P, ((first + i) % 2 + 1) * P)
@@ -230,60 +210,96 @@ def tile_attend_at_resid_topk_kernel(tc, qT, k_words, k_scales, c_words, c_scale
                     start=True,
                     stop=True,
                 )
+            return sums
 
-        listed_first = gather_values(0, N)
-        y_pairs = [stage.tile([P, 2, P, PACK], BF16, name="y_pair_%d" % h, offset=h * 4 * N, align_bytes=64) for h in range(2)]
+        out_rows = out[0].rearrange("(m q) e -> q m e", q=P)
+
+        def queries_of(o, first):
+            grouped = [group_queries(o, first, 1, False), group_queries(o, first + 1, 1, (o, first) != (0, 0))]
+            for i in range(2):
+                quantise_queries(o, first + i, 1, grouped[i])
+
+        key_codes = [gather_words("k", k_pool)]
+        queries_of(0, 0)
+        key_codes.append(gather_words("c", c_pool))
+        for table in range(2):
+            for m in range(2):
+                score_pass(m, table, 0, start=(table == 0))
+        queries_of(1, 0)
+        for m in range(2):
+            for table in range(2):
+                score_pass(m, table, 1, stop=(table == 1))
+        queries_of(0, 2)
+        for m in range(2, Q_TILES):
+            for table in range(2):
+                score_pass(m, table, 0, start=(table == 0))
+        grouped = [group_queries(1, 2, 1, True), group_queries(1, 3, 1, False)]
+        for m in range(2, Q_TILES):
+            quantise_queries(1, m, 1, grouped[m - 2])
+            for table in range(2):
+                score_pass(m, table, 1, stop=(table == 1))
+        dealt = [exp_scores(m, AT_LAST_Q + m * 4 * N) for m in range(2)]
+        dealt = dealt + [exp_scores(m) for m in range(2, Q_TILES)]
+        y_turned = [turn_weights(m, dealt[m], "x%d" % m) for m in range(Q_TILES)]
+        listed = gather_values(0, N)
+        y_pairs = [keep.tile([P, 2, P, PACK], BF16, name="y_pair_%d" % h, align_bytes=64) for h in range(2)]
         for m in range(Q_TILES):
-            scale_weights(m, y_pairs[m // 2])
-        y_mx = [quantise_weights(h, y_pairs[h]) for h in range(2)]
+            scale_weights(y_turned[m], y_pairs[m // 2][:, m % 2])
+        y_mx = [quantise("y_%d" % h, y_pairs[h][:].rearrange("s m q t -> s (m q t)"), 2 * P) for h in range(2)]
+        turned_first = turn_values(0, listed, "s0")
 
-        listed_second = gather_values(1, 0)
-        early = stage.tile([P, 2, N], BF16, name="v_grouped_early", offset=SLOT, align_bytes=64)
-        turn_values(0, listed_first, early[:, 0, :], False)
-        turn_values(1, listed_second, early[:, 1, :], True)
-        warm = psum.tile([P, NQ], F32, name="warm", tag="turned_0")
-        for o in range(PASSES):
+        def warm_up(name, codes, plane):
+            warm = psum.tile([P, NQ], F32, name=name, tag="x3")
             nc.tensor.matmul_mx(
                 out=warm[:],
-                lhsT=q_codes[o][:, 0:P].bitcast(FP8X4),
-                lhsT_scale=q_planes[o][:, 0:P],
-                rhs=q_codes[o][:].bitcast(FP8X4),
-                rhs_scale=q_planes[o][:],
-                start=(o == 0),
-                stop=(o == PASSES - 1),
+                lhsT=codes[:, 0:P].bitcast(FP8X4),
+                lhsT_scale=plane[:, 0:P],
+                rhs=q_codes[0][:].bitcast(FP8X4),
+                rhs_scale=q_planes[0][:],
+                start=True,
+                stop=True,
             )
-        listed_third = gather_values(2, 0)
-        third = keep.tile([P, N], BF16, name="v_grouped_third", align_bytes=64)
-        turn_values(2, listed_third, third[:], False)
-        v_early = quantise("v_early", early[:].rearrange("s j c -> s (j c)"), 2 * P, 2 * SLOT)
-        sums_early = []
-        for h in range(2):
-            sums_early.append(psum.tile([P, 2, 2 * P], F32, name="sums_early_%d" % h, tag="scores_%d" % h))
-            products(v_early, sums_early[h], 2 * h, 2)
 
-        listed_last = gather_values(3, 5 * N // 8)
-        v_third = quantise("v_third", third[:], P, 3 * SLOT)
-        staged_a = stage.tile([P, 2, 2 * P], F32, name="staged_a", offset=3 * SLOT + 8 * N)
-        nc.vector.tensor_copy(staged_a[:], sums_early[0][:])
-        nc.sync.dma_start(out_rows[:, 0:2, 0 : 2 * P], staged_a[:])
-        staged_b = stage.tile([P, 2, 2 * P], F32, name="staged_b", offset=3 * SLOT + 4 * N)
-        nc.scalar.copy(staged_b[:], sums_early[1][:])
-        nc.sync.dma_start(out_rows[:, 2:4, 0 : 2 * P], staged_b[:])
-        last = keep.tile([P, N], BF16, name="v_grouped_last", align_bytes=64)
-        turn_values(3, listed_last, last[:], False)
-        v_last = quantise("v_last", last[:], P)
-        sums_third = psum.tile([P, Q_TILES, P], F32, name="sums_third", tag="scores_2")
-        products(v_third, sums_third, 0, Q_TILES)
-        staged_third = keep.tile([P, Q_TILES, P], F32, name="staged_third")
-        nc.scalar.copy(staged_third[:], sums_third[:])
-        nc.sync.dma_start(out_rows[:, :, 2 * P : 3 * P], staged_third[:])
-        low = psum.tile([P, 2, P], F32, name="low", tag="scores_3")
-        products(v_last, low, 0, 2)
-        high = psum.tile([P, 2, P], F32, name="high", tag="scores_0")
-        products(v_last, high, 2, 2)
-        staged_low = keep.tile([P, 2, P], F32, name="staged_low")
-        nc.vector.tensor_copy(staged_low[:], low[:])
-        nc.sync.dma_start(out_rows[:, 0:2, 3 * P : 4 * P], staged_low[:])
-        staged_high = keep.tile([P, 2, P], F32, name="staged_high")
-        nc.scalar.copy(staged_high[:], high[:])
-        nc.scalar.dma_start(out_rows[:, 2:4, 3 * P : 4 * P], staged_high[:])
+        def store(j, staged, first, count):
+            nc.sync.dma_start(out_rows[:, first : first + count, j * P : (j + 1) * P], staged)
+
+        warm_up("warm_first", q_codes[1], q_planes[1])
+        listed = gather_values(1, 0)
+        first = stage.tile([P, N], BF16, name="v_grouped_first", offset=SLOT, align_bytes=64)
+        group_values(first[:], turned_first, False)
+        sums_first = products("sums_first", quantise("v_first", first[:], P), 0, Q_TILES, "x0")
+        turned = turn_values(1, listed, "s1")
+        listed = gather_values(2, THIRD_SHARED)
+        second = stage.tile([P, N], BF16, name="v_grouped_second", offset=2 * SLOT, align_bytes=64)
+        group_values(second[:], turned, False)
+        staged = stage.tile([P, Q_TILES, P], F32, name="staged_first", offset=2 * SLOT + 4 * N)
+        nc.vector.tensor_copy(staged[:], sums_first[:])
+        store(0, staged[:], 0, Q_TILES)
+        third = keep.tile([P, N], BF16, name="v_grouped_third", align_bytes=64)
+        group_values(third[:], turn_values(2, listed, "s2"), False)
+        v_mx = quantise("v_second", second[:], P)
+        sums_second = [products("sums_second_%d" % h, v_mx, 2 * h, 2, "x%d" % (h + 1)) for h in range(2)]
+        warm_up("warm_second", v_mx[0], v_mx[1])
+        listed = gather_values(3, SHARED)
+        turned = turn_values(3, listed, "s3")
+        v_mx = quantise("v_third", third[:], P, 3 * SLOT)
+        sums_third = [products("sums_third_%d" % h, v_mx, 2 * h, 2, "s%d" % h) for h in range(2)]
+        staged = stage.tile([P, Q_TILES, P], F32, name="staged_second", offset=3 * SLOT + 4 * N)
+        nc.vector.tensor_copy(staged[:, 0:2, :], sums_second[0][:])
+        nc.scalar.copy(staged[:, 2:4, :], sums_second[1][:])
+        store(1, staged[:], 0, Q_TILES)
+        last = stage.tile([P, N], BF16, name="v_grouped_last", offset=AT_LAST_GROUPED, align_bytes=64)
+        group_values(last[:], turned, False)
+        v_mx = quantise("v_last", last[:], P)
+        low = keep.tile([P, 2, P], F32, name="staged_third_low")
+        nc.scalar.copy(low[:], sums_third[0][:])
+        store(2, low[:], 0, 2)
+        high = stage.tile([P, 2, P], F32, name="staged_third_high", offset=AT_LAST_GROUPED)
+        nc.vector.tensor_copy(high[:], sums_third[1][:])
+        store(2, high[:], 2, 2)
+        sums_last = [products("sums_last_%d" % h, v_mx, 2 * h, 2, ("x0", "s2")[h]) for h in range(2)]
+        staged = keep.tile([P, Q_TILES, P], F32, name="staged_last")
+        nc.vector.tensor_copy(staged[:, 0:2, :], sums_last[0][:])
+        store(3, staged[:, 0:2, :], 0, 2)
+        nc.scalar.copy(staged[:, 2:4, :], sums_last[1][:])
+        store(3, staged[:, 2:4, :], 2, 2)

@@ -240,13 +240,19 @@ def tile_attend_at_resid_topk_kernel(tc, qT, k_words, k_scales, c_words, c_scale
                 score_pass(m, table, 1, stop=(table == 1))
         dealt = [exp_scores(m, AT_LAST_Q + m * 4 * N) for m in range(2)]
         dealt = dealt + [exp_scores(m) for m in range(2, Q_TILES)]
-        y_turned = [turn_weights(m, dealt[m], "x%d" % m) for m in range(Q_TILES)]
+        y_turned = [turn_weights(m, dealt[m], "x%d" % m) for m in range(2)]
         listed = gather_values(0, N)
+        y_turned = y_turned + [turn_weights(m, dealt[m], "x%d" % m) for m in range(2, Q_TILES)]
+        turned = turn_values(0, listed, "s0")
         y_pairs = [keep.tile([P, 2, P, PACK], BF16, name="y_pair_%d" % h, align_bytes=64) for h in range(2)]
         for m in range(Q_TILES):
             scale_weights(y_turned[m], y_pairs[m // 2][:, m % 2])
-        y_mx = [quantise("y_%d" % h, y_pairs[h][:].rearrange("s m q t -> s (m q t)"), 2 * P) for h in range(2)]
-        turned_first = turn_values(0, listed, "s0")
+        y_mx = [quantise("y_0", y_pairs[0][:].rearrange("s m q t -> s (m q t)"), 2 * P)]
+        listed = gather_values(1, 0)
+        y_mx.append(quantise("y_1", y_pairs[1][:].rearrange("s m q t -> s (m q t)"), 2 * P, SLOT))
+        first = stage.tile([P, N], BF16, name="v_grouped_first", offset=SLOT + 2 * N, align_bytes=64)
+        group_values(first[:], turned, False)
+        v_mx = quantise("v_first", first[:], P)
 
         def warm_up(name, codes, plane):
             warm = psum.tile([P, NQ], F32, name=name, tag="x3")
@@ -263,30 +269,35 @@ def tile_attend_at_resid_topk_kernel(tc, qT, k_words, k_scales, c_words, c_scale
         def store(j, staged, first, count):
             nc.sync.dma_start(out_rows[:, first : first + count, j * P : (j + 1) * P], staged)
 
-        warm_up("warm_first", q_codes[1], q_planes[1])
-        listed = gather_values(1, 0)
-        first = stage.tile([P, N], BF16, name="v_grouped_first", offset=SLOT, align_bytes=64)
-        group_values(first[:], turned_first, False)
-        sums_first = products("sums_first", quantise("v_first", first[:], P), 0, Q_TILES, "x0")
-        turned = turn_values(1, listed, "s1")
+        def multiply(name, v_mx, tags):
+            count = Q_TILES // len(tags)
+            return [products("%s_%d" % (name, h), v_mx, count * h, count, tag) for h, tag in enumerate(tags)]
+
+        def copy_halves(staged, sums):
+            nc.vector.tensor_copy(staged[:, 0:2, :], sums[0][:])
+            nc.scalar.copy(staged[:, 2:4, :], sums[1][:])
+
+        turned_second = turn_values(1, listed, "s1")
+        warm_up("warm_first", y_mx[1][0], y_mx[1][1])
+        sums = multiply("sums_first", v_mx, ("x0", "x1"))
         listed = gather_values(2, THIRD_SHARED)
+        turned = turn_values(2, listed, "s2")
         second = stage.tile([P, N], BF16, name="v_grouped_second", offset=2 * SLOT, align_bytes=64)
-        group_values(second[:], turned, False)
+        group_values(second[:], turned_second, False)
+        v_mx = quantise("v_second", second[:], P)
         staged = stage.tile([P, Q_TILES, P], F32, name="staged_first", offset=2 * SLOT + 4 * N)
-        nc.vector.tensor_copy(staged[:], sums_first[:])
+        copy_halves(staged, sums)
         store(0, staged[:], 0, Q_TILES)
         third = keep.tile([P, N], BF16, name="v_grouped_third", align_bytes=64)
-        group_values(third[:], turn_values(2, listed, "s2"), False)
-        v_mx = quantise("v_second", second[:], P)
-        sums_second = [products("sums_second_%d" % h, v_mx, 2 * h, 2, "x%d" % (h + 1)) for h in range(2)]
+        group_values(third[:], turned, False)
+        sums_second = multiply("sums_second", v_mx, ("x2", "s0"))
         warm_up("warm_second", v_mx[0], v_mx[1])
         listed = gather_values(3, SHARED)
         turned = turn_values(3, listed, "s3")
         v_mx = quantise("v_third", third[:], P, 3 * SLOT)
-        sums_third = [products("sums_third_%d" % h, v_mx, 2 * h, 2, "s%d" % h) for h in range(2)]
+        sums_third = multiply("sums_third", v_mx, ("s1", "x0"))
         staged = stage.tile([P, Q_TILES, P], F32, name="staged_second", offset=3 * SLOT + 4 * N)
-        nc.vector.tensor_copy(staged[:, 0:2, :], sums_second[0][:])
-        nc.scalar.copy(staged[:, 2:4, :], sums_second[1][:])
+        copy_halves(staged, sums_second)
         store(1, staged[:], 0, Q_TILES)
         last = stage.tile([P, N], BF16, name="v_grouped_last", offset=AT_LAST_GROUPED, align_bytes=64)
         group_values(last[:], turned, False)
@@ -297,9 +308,9 @@ def tile_attend_at_resid_topk_kernel(tc, qT, k_words, k_scales, c_words, c_scale
         high = stage.tile([P, 2, P], F32, name="staged_third_high", offset=AT_LAST_GROUPED)
         nc.vector.tensor_copy(high[:], sums_third[1][:])
         store(2, high[:], 2, 2)
-        sums_last = [products("sums_last_%d" % h, v_mx, 2 * h, 2, ("x0", "s2")[h]) for h in range(2)]
+        sums = multiply("sums_last", v_mx, ("x1", "s2", "x3", "x2"))
         staged = keep.tile([P, Q_TILES, P], F32, name="staged_last")
-        nc.vector.tensor_copy(staged[:, 0:2, :], sums_last[0][:])
-        store(3, staged[:, 0:2, :], 0, 2)
-        nc.scalar.copy(staged[:, 2:4, :], sums_last[1][:])
-        store(3, staged[:, 2:4, :], 2, 2)
+        for h in range(2):
+            nc.scalar.copy(staged[:, 2 * h : 2 * h + 1, :], sums[2 * h][:])
+            nc.vector.tensor_copy(staged[:, 2 * h + 1 : 2 * h + 2, :], sums[2 * h + 1][:])
+            store(3, staged[:, 2 * h : 2 * h + 2, :], 2 * h, 2)

@@ -27,7 +27,7 @@ SLOT = 4 * T
 SCALE_ROWS = 32
 FIRST_ROW = P - SCALE_ROWS
 SHARED = 5 * N // 8
-THIRD_SHARED = N // 2
+THIRD_SHARED = 7 * N // 16
 AT_Q = E_TILES * SLOT
 Q_BYTES = 4 * PACK * HALF
 AT_LAST_Q = AT_Q + 3 * Q_BYTES
@@ -254,12 +254,12 @@ def tile_attend_at_resid_topk_kernel(tc, qT, k_words, k_scales, c_words, c_scale
         group_values(first[:], turned, False)
         v_mx = quantise("v_first", first[:], P)
 
-        def warm_up(name, codes, plane):
-            warm = psum.tile([P, NQ], F32, name=name, tag="x3")
+        def warm_up(name, tag):
+            warm = psum.tile([P, NQ], F32, name=name, tag=tag)
             nc.tensor.matmul_mx(
                 out=warm[:],
-                lhsT=codes[:, 0:P].bitcast(FP8X4),
-                lhsT_scale=plane[:, 0:P],
+                lhsT=q_codes[1][:, 0:P].bitcast(FP8X4),
+                lhsT_scale=q_planes[1][:, 0:P],
                 rhs=q_codes[0][:].bitcast(FP8X4),
                 rhs_scale=q_planes[0][:],
                 start=True,
@@ -278,7 +278,7 @@ def tile_attend_at_resid_topk_kernel(tc, qT, k_words, k_scales, c_words, c_scale
             nc.scalar.copy(staged[:, 2:4, :], sums[1][:])
 
         turned_second = turn_values(1, listed, "s1")
-        warm_up("warm_first", y_mx[1][0], y_mx[1][1])
+        warm_up("warm_first", "s0")
         sums = multiply("sums_first", v_mx, ("x0", "x1"))
         listed = gather_values(2, THIRD_SHARED)
         turned = turn_values(2, listed, "s2")
@@ -290,8 +290,8 @@ def tile_attend_at_resid_topk_kernel(tc, qT, k_words, k_scales, c_words, c_scale
         store(0, staged[:], 0, Q_TILES)
         third = keep.tile([P, N], BF16, name="v_grouped_third", align_bytes=64)
         group_values(third[:], turned, False)
+        warm_up("warm_second", "x0")
         sums_second = multiply("sums_second", v_mx, ("x2", "s0"))
-        warm_up("warm_second", v_mx[0], v_mx[1])
         listed = gather_values(3, SHARED)
         turned = turn_values(3, listed, "s3")
         v_mx = quantise("v_third", third[:], P, 3 * SLOT)

@@ -26,7 +26,7 @@ LIST_COLS = N // 16
 SLOT = 4 * T
 SCALE_ROWS = 32
 FIRST_ROW = P - SCALE_ROWS
-SHARED = 5 * N // 8
+SHARED = 11 * N // 16
 THIRD_SHARED = 7 * N // 16
 AT_Q = E_TILES * SLOT
 Q_BYTES = 4 * PACK * HALF

@@ -26,7 +26,7 @@ LIST_COLS = N // 16
 SLOT = 4 * T
 SCALE_ROWS = 32
 FIRST_ROW = P - SCALE_ROWS
-SHARED = 11 * N // 16
+SHARED = 3 * N // 4
 THIRD_SHARED = 7 * N // 16
 AT_Q = E_TILES * SLOT
 Q_BYTES = 4 * PACK * HALF
@@ -254,14 +254,14 @@ def tile_attend_at_resid_topk_kernel(tc, qT, k_words, k_scales, c_words, c_scale
         group_values(first[:], turned, False)
         v_mx = quantise("v_first", first[:], P)
 
-        def warm_up(name, tag):
-            warm = psum.tile([P, NQ], F32, name=name, tag=tag)
+        def warm_up(name, tag, width):
+            warm = psum.tile([P, width], F32, name=name, tag=tag)
             nc.tensor.matmul_mx(
                 out=warm[:],
                 lhsT=q_codes[1][:, 0:P].bitcast(FP8X4),
                 lhsT_scale=q_planes[1][:, 0:P],
-                rhs=q_codes[0][:].bitcast(FP8X4),
-                rhs_scale=q_planes[0][:],
+                rhs=q_codes[0][:, 0:width].bitcast(FP8X4),
+                rhs_scale=q_planes[0][:, 0:width],
                 start=True,
                 stop=True,
             )
@@ -278,7 +278,7 @@ def tile_attend_at_resid_topk_kernel(tc, qT, k_words, k_scales, c_words, c_scale
             nc.scalar.copy(staged[:, 2:4, :], sums[1][:])
 
         turned_second = turn_values(1, listed, "s1")
-        warm_up("warm_first", "s0")
+        warm_up("warm_first", "s0", NQ)
         sums = multiply("sums_first", v_mx, ("x0", "x1"))
         listed = gather_values(2, THIRD_SHARED)
         turned = turn_values(2, listed, "s2")
@@ -290,7 +290,7 @@ def tile_attend_at_resid_topk_kernel(tc, qT, k_words, k_scales, c_words, c_scale
         store(0, staged[:], 0, Q_TILES)
         third = keep.tile([P, N], BF16, name="v_grouped_third", align_bytes=64)
         group_values(third[:], turned, False)
-        warm_up("warm_second", "x0")
+        warm_up("warm_second", "x0", NQ // 2)
         sums_second = multiply("sums_second", v_mx, ("x2", "s0"))
         listed = gather_values(3, SHARED)
         turned = turn_values(3, listed, "s3")

@@ -26,8 +26,8 @@ LIST_COLS = N // 16
 SLOT = 4 * T
 SCALE_ROWS = 32
 FIRST_ROW = P - SCALE_ROWS
-SHARED = 3 * N // 4
-THIRD_SHARED = 7 * N // 16
+SHARED = 11 * N // 16
+THIRD_SHARED = 3 * N // 8
 AT_Q = E_TILES * SLOT
 Q_BYTES = 4 * PACK * HALF
 AT_LAST_Q = AT_Q + 3 * Q_BYTES
@@ -214,23 +214,37 @@ def tile_attend_at_resid_topk_kernel(tc, qT, k_words, k_scales, c_words, c_scale
 
         out_rows = out[0].rearrange("(m q) e -> q m e", q=P)
 
-        def queries_of(o, first):
-            grouped = [group_queries(o, first, 1, False), group_queries(o, first + 1, 1, (o, first) != (0, 0))]
-            for i in range(2):
-                quantise_queries(o, first + i, 1, grouped[i])
+        def warm_up(name, tag, o, width):
+            warm = psum.tile([P, width], F32, name=name, tag=tag)
+            nc.tensor.matmul_mx(
+                out=warm[:],
+                lhsT=q_codes[o][:, 0:P].bitcast(FP8X4),
+                lhsT_scale=q_planes[o][:, 0:P],
+                rhs=q_codes[0][:, 0:width].bitcast(FP8X4),
+                rhs_scale=q_planes[0][:, 0:width],
+                start=True,
+                stop=True,
+            )
+
+        def queries_of(o):
+            grouped = [group_queries(o, m, 1, (o, m) == (0, 1)) for m in range(2)]
+            for m in range(2):
+                quantise_queries(o, m, 1, grouped[m])
 
         key_codes = [gather_words("k", k_pool)]
-        queries_of(0, 0)
+        queries_of(0)
+        warm_up("warm_head", "x1", 0, NQ // 2)
         key_codes.append(gather_words("c", c_pool))
         for table in range(2):
             for m in range(2):
                 score_pass(m, table, 0, start=(table == 0))
-        queries_of(1, 0)
+        queries_of(1)
         for m in range(2):
             for table in range(2):
                 score_pass(m, table, 1, stop=(table == 1))
-        queries_of(0, 2)
-        for m in range(2, Q_TILES):
+        grouped = [group_queries(0, 2, 1, False), group_queries(0, 3, 1, True)]
+        for m in (3, 2):
+            quantise_queries(0, m, 1, grouped[m - 2])
             for table in range(2):
                 score_pass(m, table, 0, start=(table == 0))
         grouped = [group_queries(1, 2, 1, True), group_queries(1, 3, 1, False)]
@@ -254,18 +268,6 @@ def tile_attend_at_resid_topk_kernel(tc, qT, k_words, k_scales, c_words, c_scale
         group_values(first[:], turned, False)
         v_mx = quantise("v_first", first[:], P)
 
-        def warm_up(name, tag, width):
-            warm = psum.tile([P, width], F32, name=name, tag=tag)
-            nc.tensor.matmul_mx(
-                out=warm[:],
-                lhsT=q_codes[1][:, 0:P].bitcast(FP8X4),
-                lhsT_scale=q_planes[1][:, 0:P],
-                rhs=q_codes[0][:, 0:width].bitcast(FP8X4),
-                rhs_scale=q_planes[0][:, 0:width],
-                start=True,
-                stop=True,
-            )
-
         def store(j, staged, first, count):
             nc.sync.dma_start(out_rows[:, first : first + count, j * P : (j + 1) * P], staged)
 
@@ -278,7 +280,7 @@ def tile_attend_at_resid_topk_kernel(tc, qT, k_words, k_scales, c_words, c_scale
             nc.scalar.copy(staged[:, 2:4, :], sums[1][:])
 
         turned_second = turn_values(1, listed, "s1")
-        warm_up("warm_first", "s0", NQ)
+        warm_up("warm_first", "s0", 1, NQ)
         sums = multiply("sums_first", v_mx, ("x0", "x1"))
         listed = gather_values(2, THIRD_SHARED)
         turned = turn_values(2, listed, "s2")
@@ -290,7 +292,7 @@ def tile_attend_at_resid_topk_kernel(tc, qT, k_words, k_scales, c_words, c_scale
         store(0, staged[:], 0, Q_TILES)
         third = keep.tile([P, N], BF16, name="v_grouped_third", align_bytes=64)
         group_values(third[:], turned, False)
-        warm_up("warm_second", "x0", NQ // 2)
+        warm_up("warm_second", "x0", 1, NQ // 2)
         sums_second = multiply("sums_second", v_mx, ("x2", "s0"))
         listed = gather_values(3, SHARED)
         turned = turn_values(3, listed, "s3")

@@ -27,7 +27,7 @@ SLOT = 4 * T
 SCALE_ROWS = 32
 FIRST_ROW = P - SCALE_ROWS
 SHARED = 11 * N // 16
-THIRD_SHARED = 3 * N // 8
+THIRD_SHARED = 7 * N // 16
 AT_Q = E_TILES * SLOT
 Q_BYTES = 4 * PACK * HALF
 AT_LAST_Q = AT_Q + 3 * Q_BYTES
@@ -233,7 +233,6 @@ def tile_attend_at_resid_topk_kernel(tc, qT, k_words, k_scales, c_words, c_scale
 
         key_codes = [gather_words("k", k_pool)]
         queries_of(0)
-        warm_up("warm_head", "x1", 0, NQ // 2)
         key_codes.append(gather_words("c", c_pool))
         for table in range(2):
             for m in range(2):
@@ -292,7 +291,7 @@ def tile_attend_at_resid_topk_kernel(tc, qT, k_words, k_scales, c_words, c_scale
         store(0, staged[:], 0, Q_TILES)
         third = keep.tile([P, N], BF16, name="v_grouped_third", align_bytes=64)
         group_values(third[:], turned, False)
-        warm_up("warm_second", "x0", 1, NQ // 2)
+        warm_up("warm_second", "x0", 1, NQ)
         sums_second = multiply("sums_second", v_mx, ("x2", "s0"))
         listed = gather_values(3, SHARED)
         turned = turn_values(3, listed, "s3")

from contextlib import ExitStack

import concourse.mybir as mybir
from concourse.masks import make_identity

F32 = mybir.dt.float32
BF16 = mybir.dt.bfloat16
I32 = mybir.dt.int32
U32 = mybir.dt.uint32
U16 = mybir.dt.uint16
U8 = mybir.dt.uint8
FP8X4 = mybir.dt.float8_e4m3fn_x4
FP4X4 = mybir.dt.float4_e2m1fn_x4
EXP = mybir.ActivationFunctionType.Exp
COPY = mybir.ActivationFunctionType.Copy
MULT = mybir.AluOpType.mult

P = 128
PACK = 4
N, T, D, NQ, DV = 512, 2048, 1024, 512, 512
PASSES = D // (P * PACK)
Q_TILES = NQ // P
E_TILES = DV // P
HALF = NQ // 2
LIST_COLS = N // 16
SLOT = 4 * T
SCALE_ROWS = 32
FIRST_ROW = P - SCALE_ROWS
SHARED = 11 * N // 16
THIRD_SHARED = 7 * N // 16
AT_Q = E_TILES * SLOT
Q_BYTES = 4 * PACK * HALF
AT_LAST_Q = AT_Q + 3 * Q_BYTES
AT_LISTED = AT_Q + 4 * Q_BYTES
AT_LAST_GROUPED = AT_LISTED + E_TILES * 2 * N

FLOPS = 2 * N * NQ * (2 * D + DV)


def tile_attend_at_resid_topk_kernel(tc, qT, k_words, k_scales, c_words, c_scales, vT, ls, us, offs, out):
    nc = tc.nc
    with ExitStack() as ctx:
        keep = ctx.enter_context(tc.tile_pool(name="keep", bufs=1))
        stage = ctx.enter_context(tc.tile_pool(name="stage", bufs=1))
        psum = ctx.enter_context(tc.psum_pool(name="psum", bufs=1))

        offsets = keep.tile([P, LIST_COLS], U16, name="offsets")
        nc.sync.dma_start(offsets[:], offs)

        def load_bytes(name, scales):
            pool_bytes = keep.tile([P, T], U8, name=name + "_pool_bytes")
            nc.sync.dma_start(pool_bytes[FIRST_ROW:P, :].bitcast(I32), scales.rearrange("o f t -> f o t").bitcast(I32))
            nc.vector.memset(pool_bytes[0:FIRST_ROW, :].bitcast(I32), 0)
            return pool_bytes

        def load_words(name, words):
            pool_words = keep.tile([P, T], I32, name=name + "_pool_words")
            nc.sync.dma_start(pool_words[:], words[0].rearrange("p t b -> p (t b)").bitcast(I32))
            return pool_words

        def load_queries(o, h):
            raw = stage.tile([P, PACK, HALF], F32, name="q_raw_%d_%d" % (o, h), offset=AT_Q + (2 * h + o) * Q_BYTES)
            rows = qT[0, o * P * PACK : (o + 1) * P * PACK, h * HALF : (h + 1) * HALF]
            nc.sync.dma_start(raw[:], rows.rearrange("(p j) c -> p j c", j=PACK))
            return raw

        def load_values(j):
            v_pool = stage.tile([P, T], F32, name="v_pool_%d" % j, offset=j * SLOT)
            nc.sync.dma_start(v_pool[:], vT[j * P : (j + 1) * P, :])
            return v_pool

        byte_pools = [load_bytes("k", k_scales), load_bytes("c", c_scales)]
        identity = keep.tile([P, P], F32, name="identity")
        make_identity(nc, identity[:])
        padded = keep.tile([P, P], F32, name="padded")
        nc.gpsimd.memset(padded[:], 0.0)
        nc.gpsimd.dma_start(padded[0:Q_TILES, :], ls[0, 0].rearrange("(m p) -> m p", p=P))
        us_cols = keep.tile([P, PACK], F32, name="us_cols")
        nc.gpsimd.dma_start(us_cols[:], us[0].rearrange("(p t) one -> p (t one)", t=PACK))

        k_pool = load_words("k", k_words)
        q_raw = {(0, 0): load_queries(0, 0)}
        c_pool = load_words("c", c_words)

        listed_bytes = keep.tile([P, 2, N], U8, name="listed_bytes", align_bytes=64)
        planes = keep.tile([P, PASSES, 2, N], U8, name="planes", align_bytes=64)
        nc.vector.memset(planes[:].rearrange("p o t n -> p (o t n)").bitcast(I32), 0)
        for table in range(2):
            nc.vector.tensor_copy(listed_bytes[:, table, :], byte_pools[table][:].indirect(offsets[:]))
        for quad in (0, 2, 1, 3):
            nc.sync.dma_start(
                planes[32 * quad : 32 * quad + 4].rearrange("p o t n -> p o (t n)").bitcast(I32),
                listed_bytes[FIRST_ROW + 8 * quad : FIRST_ROW + 8 * quad + 8].rearrange("p t n -> p (t n)").bitcast(I32),
            )
        for o, h in ((1, 0), (0, 1), (1, 1)):
            q_raw[o, h] = load_queries(o, h)
        v_pools = [load_values(j) for j in range(E_TILES)]

        ls_turned = psum.tile([P, P], F32, name="ls_turned", tag="x0")
        nc.tensor.transpose(ls_turned[:], padded[:], identity[:])
        neg_ls = keep.tile([P, Q_TILES], F32, name="neg_ls")
        nc.scalar.activation(neg_ls[:], ls_turned[:, 0:Q_TILES], COPY, scale=-1.0)

        def gather_words(name, pool_words):
            listed_words = keep.tile([P, N], U32, name=name + "_listed_words")
            nc.vector.tensor_copy(listed_words[:], pool_words[:].bitcast(U32).indirect(offsets[:]))
            halves = []
            for o in range(PASSES):
                half = keep.tile([P, N], U16, name=name + "_half_%d" % o, align_bytes=64)
                nc.vector.tensor_copy(half[:], listed_words[:].bitcast(U16)[:, o : PASSES * N : PASSES])
                halves.append(half)
            return halves

        q_codes = [keep.tile([P, NQ], U32, name="q_codes_%d" % o, align_bytes=64) for o in range(PASSES)]
        q_planes = [keep.tile([P, NQ], U8, name="q_plane_%d" % o, align_bytes=64) for o in range(PASSES)]

        def group_queries(o, first, count, on_vector):
            grouped = keep.tile([P, count * P, PACK], BF16, name="q_grouped_%d_%d" % (o, first), align_bytes=64)
            at = first % 2 * P
            part = q_raw[o, first // 2][:, :, at : at + count * P].rearrange("p j c -> p c j")
            if on_vector:
                nc.vector.tensor_copy(grouped[:], part)
            else:
                nc.scalar.copy(grouped[:], part)
            return grouped

        def quantise_queries(o, first, count, grouped):
            cols = slice(first * P, (first + count) * P)
            nc.vector.quantize_mx(
                out=q_codes[o][:, cols].bitcast(FP8X4), scales=q_planes[o][:, cols], in_=grouped[:].rearrange("p c j -> p (c j)")
            )

        banks = [psum.tile([P, N], F32, name="scores_%d" % m, tag="s%d" % m) for m in range(Q_TILES)]

        def score_pass(m, table, o, start=False, stop=False):
            cols = slice(m * P, (m + 1) * P)
            nc.tensor.matmul_mx(
                out=banks[m][:],
                lhsT=q_codes[o][:, cols].bitcast(FP8X4),
                lhsT_scale=q_planes[o][:, cols],
                rhs=key_codes[table][o][:].bitcast(FP4X4),
                rhs_scale=planes[:, o, table, :],
                start=start,
                stop=stop,
            )

        def exp_scores(m, at=None):
            if at is None:
                dealt = keep.tile([P, PACK, P], F32, name="dealt_%d" % m)
            else:
                dealt = stage.tile([P, PACK, P], F32, name="dealt_%d" % m, offset=at)
            nc.scalar.activation(dealt[:], banks[m][:].rearrange("q (s t) -> q t s", t=PACK), EXP, bias=neg_ls[:, m : m + 1])
            return dealt

        def turn_weights(m, dealt, tag):
            turned = psum.tile([P, PACK, P], F32, name="y_turned_%d" % m, tag=tag)
            for t in range(PACK):
                nc.tensor.transpose(turned[:, t, :], dealt[:, t, :], identity[:])
            return turned

        def scale_weights(turned, grouped):
            nc.vector.tensor_tensor(
                grouped, turned[:].rearrange("s t q -> s q t"), us_cols[:].unsqueeze(1).to_broadcast([P, P, PACK]), MULT
            )

        def quantise(name, grouped, width, at=None):
            if at is None:
                codes = keep.tile([P, width], U32, name=name + "_codes", align_bytes=64)
            else:
                codes = stage.tile([P, width], U32, name=name + "_codes", offset=at, align_bytes=64)
            plane = keep.tile([P, width], U8, name=name + "_plane", align_bytes=64)
            nc.vector.quantize_mx(out=codes[:].bitcast(FP8X4), scales=plane[:], in_=grouped)
            return codes, plane

        def gather_values(j, on_vector):
            listed_v = stage.tile([P, N], BF16, name="listed_v_%d" % j, offset=AT_LISTED + j * 2 * N)
            cut = on_vector // 16
            if on_vector > 0:
                nc.vector.tensor_copy(listed_v[:, 0:on_vector], v_pools[j][:].indirect(offsets[:, 0:cut]))
            if on_vector < N:
                nc.scalar.activation(listed_v[:, on_vector:N], v_pools[j][:].indirect(offsets[:, cut:LIST_COLS]), COPY)
            return listed_v

        def turn_values(j, listed_v, tag):
            pairs = listed_v[:].bitcast(F32)
            turned = psum.tile([P, 2, P], F32, name="v_turned_%d" % j, tag=tag)
            for u in range(2):
                nc.tensor.transpose(turned[:, u, :], pairs[:, u : N // 2 : 2], identity[:])
            return turned

        def group_values(grouped, turned, on_vector):
            words = grouped.bitcast(F32).rearrange("s (e u) -> s e u", u=2)
            if on_vector:
                nc.vector.tensor_copy(words, turned[:].rearrange("s u e -> s e u"))
            else:
                nc.scalar.copy(words, turned[:].rearrange("s u e -> s e u"))

        def products(name, v_mx, first, count, tag, width=P):
            v_codes, v_plane = v_mx
            sums = psum.tile([P, count, width], F32, name=name, tag=tag)
            for i in range(count):
                codes, plane = y_mx[(first + i) // 2]
                cols = slice((first + i) % 2 * P, ((first + i) % 2 + 1) * P)
                nc.tensor.matmul_mx(
                    out=sums[:, i, :],
                    lhsT=codes[:, cols].bitcast(FP8X4),
                    lhsT_scale=plane[:, cols],
                    rhs=v_codes[:].bitcast(FP8X4),
                    rhs_scale=v_plane[:],
                    start=True,
                    stop=True,
                )
            return sums

        out_rows = out[0].rearrange("(m q) e -> q m e", q=P)

        def warm_up(name, tag, o, width):
            warm = psum.tile([P, width], F32, name=name, tag=tag)
            nc.tensor.matmul_mx(
                out=warm[:],
                lhsT=q_codes[o][:, 0:P].bitcast(FP8X4),
                lhsT_scale=q_planes[o][:, 0:P],
                rhs=q_codes[0][:, 0:width].bitcast(FP8X4),
                rhs_scale=q_planes[0][:, 0:width],
                start=True,
                stop=True,
            )

        def queries_of(o):
            grouped = [group_queries(o, m, 1, (o, m) == (0, 1)) for m in range(2)]
            for m in range(2):
                quantise_queries(o, m, 1, grouped[m])

        key_codes = [gather_words("k", k_pool)]
        queries_of(0)
        key_codes.append(gather_words("c", c_pool))
        for table in range(2):
            for m in range(2):
                score_pass(m, table, 0, start=(table == 0))
        queries_of(1)
        for m in range(2):
            for table in range(2):
                score_pass(m, table, 1, stop=(table == 1))
        grouped = [group_queries(0, 2, 1, False), group_queries(0, 3, 1, True)]
        for m in (3, 2):
            quantise_queries(0, m, 1, grouped[m - 2])
            for table in range(2):
                score_pass(m, table, 0, start=(table == 0))
        grouped = [group_queries(1, 2, 1, True), group_queries(1, 3, 1, False)]
        for m in range(2, Q_TILES):
            quantise_queries(1, m, 1, grouped[m - 2])
            for table in range(2):
                score_pass(m, table, 1, stop=(table == 1))
        dealt = [exp_scores(m, AT_LAST_Q + m * 4 * N) for m in range(2)]
        dealt = dealt + [exp_scores(m) for m in range(2, Q_TILES)]
        y_turned = [turn_weights(m, dealt[m], "x%d" % m) for m in range(2)]
        listed = gather_values(0, N)
        y_turned = y_turned + [turn_weights(m, dealt[m], "x%d" % m) for m in range(2, Q_TILES)]
        turned = turn_values(0, listed, "s0")
        y_pairs = [keep.tile([P, 2, P, PACK], BF16, name="y_pair_%d" % h, align_bytes=64) for h in range(2)]
        for m in range(Q_TILES):
            scale_weights(y_turned[m], y_pairs[m // 2][:, m % 2])
        y_mx = [quantise("y_0", y_pairs[0][:].rearrange("s m q t -> s (m q t)"), 2 * P)]
        listed = gather_values(1, 0)
        y_mx.append(quantise("y_1", y_pairs[1][:].rearrange("s m q t -> s (m q t)"), 2 * P, SLOT))
        first = stage.tile([P, N], BF16, name="v_grouped_first", offset=SLOT + 2 * N, align_bytes=64)
        group_values(first[:], turned, False)
        v_mx = quantise("v_first", first[:], P)

        def store(j, staged, first, count):
            nc.sync.dma_start(out_rows[:, first : first + count, j * P : (j + 1) * P], staged)

        def multiply(name, v_mx, tags):
            count = Q_TILES // len(tags)
            return [products("%s_%d" % (name, h), v_mx, count * h, count, tag) for h, tag in enumerate(tags)]

        def copy_halves(staged, sums):
            nc.vector.tensor_copy(staged[:, 0:2, :], sums[0][:])
            nc.scalar.copy(staged[:, 2:4, :], sums[1][:])

        turned_second = turn_values(1, listed, "s1")
        warm_up("warm_first", "s0", 1, NQ)
        sums = multiply("sums_first", v_mx, ("x0", "x1"))
        listed = gather_values(2, THIRD_SHARED)
        turned = turn_values(2, listed, "s2")
        second = stage.tile([P, N], BF16, name="v_grouped_second", offset=2 * SLOT, align_bytes=64)
        group_values(second[:], turned_second, False)
        v_mx = quantise("v_second", second[:], P)
        staged = stage.tile([P, Q_TILES, P], F32, name="staged_first", offset=2 * SLOT + 4 * N)
        copy_halves(staged, sums)
        store(0, staged[:], 0, Q_TILES)
        third = keep.tile([P, N], BF16, name="v_grouped_third", align_bytes=64)
        group_values(third[:], turned, False)
        warm_up("warm_second", "x0", 1, NQ)
        sums_second = multiply("sums_second", v_mx, ("x2", "s0"))
        listed = gather_values(3, SHARED)
        turned = turn_values(3, listed, "s3")
        v_mx = quantise("v_third", third[:], P, 3 * SLOT)
        sums_third = multiply("sums_third", v_mx, ("s1", "x0"))
        staged = stage.tile([P, Q_TILES, P], F32, name="staged_second", offset=3 * SLOT + 4 * N)
        copy_halves(staged, sums_second)
        store(1, staged[:], 0, Q_TILES)
        last = stage.tile([P, N], BF16, name="v_grouped_last", offset=AT_LAST_GROUPED, align_bytes=64)
        group_values(last[:], turned, False)
        v_mx = quantise("v_last", last[:], P)
        low = keep.tile([P, 2, P], F32, name="staged_third_low")
        nc.scalar.copy(low[:], sums_third[0][:])
        store(2, low[:], 0, 2)
        high = stage.tile([P, 2, P], F32, name="staged_third_high", offset=AT_LAST_GROUPED)
        nc.vector.tensor_copy(high[:], sums_third[1][:])
        store(2, high[:], 2, 2)
        sums = multiply("sums_last", v_mx, ("x1", "s2", "x3", "x2"))
        staged = keep.tile([P, Q_TILES, P], F32, name="staged_last")
        for h in range(2):
            nc.scalar.copy(staged[:, 2 * h : 2 * h + 1, :], sums[2 * h][:])
            nc.vector.tensor_copy(staged[:, 2 * h + 1 : 2 * h + 2, :], sums[2 * h + 1][:])
            store(3, staged[:, 2 * h : 2 * h + 2, :], 2 * h, 2)
